import numpy as np
import ml_dtypes


def mxq(x, axis, fmt="e4m3"):
    dtype, down = {"e4m3": (ml_dtypes.float8_e4m3fn, 7), "e5m2": (ml_dtypes.float8_e5m2, 14)}[fmt]
    v = np.moveaxis(np.asarray(x, np.float32).astype(ml_dtypes.bfloat16).astype(np.float64), axis, -1)
    blocks = v.reshape(v.shape[:-1] + (-1, 32))
    amax = np.abs(blocks).max(-1, keepdims=True)
    byte = np.maximum(np.where(amax > 0, np.frexp(amax)[1] - 1 + 127, 0) - down, 1)
    scale = np.exp2(byte - 127.0)
    codes = (blocks / scale).astype(np.float32).astype(dtype).astype(np.float64)
    return np.moveaxis((codes * scale).reshape(v.shape), -1, axis)


WIDE = False


def mx_kscale(k):
    if not WIDE:
        return np.ones(k)
    levels = np.array([10, -10, 5, -5, 0])
    if k % 512:
        return np.exp2(np.random.permutation(np.resize(levels, k // 32))).repeat(32)
    a = np.empty((k // 512, 16))
    for p in range(k // 512):
        a[p, :8] = np.random.permutation(np.resize(levels, 8))
        for g in range(8):
            far = levels[np.abs(levels - a[p, g]) >= 10]
            a[p, g + 8] = far[np.random.randint(len(far))]
    return np.exp2(a.ravel()).repeat(32)


BF16 = ml_dtypes.bfloat16


def bf(x):
    return np.asarray(x, np.float32).astype(BF16)


def f64(x):
    return np.asarray(x).astype(np.float64)


E2M1 = np.array([0.0, 0.5, 1.0, 1.5, 2.0, 3.0, 4.0, 6.0, -0.0, -0.5, -1.0, -1.5, -2.0, -3.0, -4.0, -6.0])


def pack_weight(w, fmt):
    k, n = w.shape
    w = f64(bf(w)).reshape(k // 32, 32, n)
    amax = np.abs(w).max(1)
    if fmt == "e4m3":
        byte = np.frexp(amax)[1] - 1 + 127 - 7
    else:
        mant, ex = np.frexp(amax / 6.0)
        byte = np.where(mant > 0.5, ex, ex - 1) + 127
    byte = np.clip(np.where(amax > 0, byte, 1), 1, 254)
    scaled = (w * np.exp2(127.0 - byte)[:, None, :]).reshape(k, n).astype(np.float32)
    by_word = np.ascontiguousarray(scaled.reshape(k // 512, 128, 4, n).transpose(0, 1, 3, 2))
    if fmt == "e4m3":
        words = by_word.astype(ml_dtypes.float8_e4m3fn).view(np.uint8)
    else:
        c = by_word.astype(ml_dtypes.float4_e2m1fn).view(np.uint8) & 0xF
        words = c[..., 0::2] | (c[..., 1::2] << 4)
    return np.ascontiguousarray(words), np.ascontiguousarray(byte.astype(np.uint8).reshape(k // 512, 16, n))


def unpack_weight(words, scales, fmt):
    g, p, n, _ = words.shape
    if fmt == "e4m3":
        vals = np.ascontiguousarray(words).view(ml_dtypes.float8_e4m3fn).astype(np.float64)
    else:
        nib = np.empty((g, p, n, 4), np.uint8)
        nib[..., 0::2] = words & 0xF
        nib[..., 1::2] = words >> 4
        vals = E2M1[nib]
    vals = vals * np.repeat(np.exp2(scales.astype(np.float64) - 127.0), 8, axis=1)[..., None]
    return vals.transpose(0, 1, 3, 2).reshape(g * 512, n)
def pack4(w):
    words, scales = pack_weight(w, "e2m1")
    return words.reshape(words.shape[0], 128, -1), scales


def unpack4(words, scales):
    return unpack_weight(words.reshape(words.shape[0], 128, -1, 2), scales, "e2m1")


def planes(Y):
    n, m = Y.shape
    b = f64(bf(Y)).reshape(n // 32, 32, m)
    amax = np.abs(b).max(1)
    byte = np.clip(np.where(amax > 0, np.frexp(amax)[1] - 1 + 127 - 7, 1), 1, 254)
    codes = (b * np.exp2(127.0 - byte)[:, None, :]).reshape(n, m).astype(np.float32).astype(ml_dtypes.float8_e4m3fn).view(np.uint8)
    words = codes.reshape(n // 512, 128, 4, m).transpose(0, 1, 3, 2)
    return np.ascontiguousarray(words), np.ascontiguousarray(byte.astype(np.uint8).reshape(n // 512, 16, m))


T, K1, K2, F, R = 2048, 1024, 512, 1024, 512

def setup_inputs():
    rnd = np.random.randn
    s1, s2, st = mx_kscale(K1), mx_kscale(K2), mx_kscale(T)
    spread = 0.7 * np.exp(0.8 * rnd(F))
    err1 = rnd(T, K1) * s1[None, :] * st[:, None]
    err2 = rnd(T, K2) * s2[None, :] * st[:, None]
    V = rnd(K1, F) * spread[None, :] / np.sqrt(K1) / s1[:, None]
    w2 = rnd(F, K2) * spread[:, None] / np.sqrt(K2) / s2[None, :]
    sample_w = np.random.exponential(size=(R, T)) / np.sqrt(T) / st[None, :]
    v_words, v_scales = pack4(V)
    return {"err1": bf(err1), "v_words": v_words, "v_scales": v_scales,
            "err2": bf(err2), "w2": bf(w2),
            "x": bf(1.0 + rnd(T, F)), "alpha": bf(np.exp(0.3 * rnd(F))),
            "sample_w": bf(sample_w), "reg": bf(0.2 + 0.3 * np.random.rand(F))}

def reference(err1, v_words, v_scales, err2, w2, x, alpha, sample_w, reg):
    x, alpha, reg = f64(x), f64(alpha), f64(reg)
    from1 = mxq(f64(err1), 1) @ unpack4(v_words, v_scales)
    from2 = mxq(f64(err2), 1) @ mxq(f64(w2), 1).T
    H = (from1 + from2) * (x >= alpha[None, :])
    y = (mxq(f64(sample_w), 1) @ mxq(H, 0)) + (reg * alpha)[None, :]
    words, scales = planes(y.T)
    return y, words, scales

@@ -1,0 +1,448 @@
+from contextlib import ExitStack
+
+import concourse.mybir as mybir
+from concourse.masks import make_identity
+
+T, K1, K2, F, R = 2048, 1024, 512, 1024, 512
+FLOPS = 2 * T * (K1 + K2) * F + 2 * R * T * F
+
+F32 = mybir.dt.float32
+BF16 = mybir.dt.bfloat16
+U8 = mybir.dt.uint8
+U32 = mybir.dt.uint32
+I32 = mybir.dt.int32
+FP8X4 = mybir.dt.float8_e4m3fn_x4
+FP4X4 = mybir.dt.float4_e2m1fn_x4
+ALU = mybir.AluOpType
+
+P = 128
+PASS = 512
+BANKS = 8
+MASK_AHEAD = [s + (1 if s >= 9 else 0) + (1 if s >= 11 else 0) for s in range(16)]
+
+
+def tile_pact_threshold_gradient_k6_kernel(
+    tc, err1, v_words, v_scales, err2, w2, x, alpha, sample_w, reg, out_0, out_1, out_2
+):
+    nc = tc.nc
+    with ExitStack() as ctx:
+        keep = ctx.enter_context(tc.tile_pool(name="keep", bufs=1))
+        stage = ctx.enter_context(tc.tile_pool(name="stage", bufs=2))
+        psum = ctx.enter_context(tc.psum_pool(name="psum", bufs=1))
+        ctx.enter_context(tc.manual_schedule())
+
+        free_banks = list(range(BANKS))
+        bank_of = {}
+
+        def take_bank(key, shape):
+            b = free_banks.pop(0)
+            bank = psum.tile(shape, F32, tag="bank%d" % b, name="bank%d" % b)
+            bank_of[key] = (b, bank)
+            return bank
+
+        def give_bank(key):
+            free_banks.append(bank_of.pop(key)[0])
+
+        def kept(name, shape, dtype):
+            return keep.tile(shape, dtype, name=name, tag=name, align_bytes=64)
+
+        ident = kept("ident", [P, P], F32)
+        make_identity(nc, ident[:])
+        v_sc = kept("v_sc", [P, 2, F], U8)
+        nc.vector.memset(v_sc[:].rearrange("p k n -> p (k n)").bitcast(I32), 0)
+
+        e1_raw, e2_raw, x_raw, sw_raw, w2_raw, v_w = {}, {}, {}, {}, {}, {}
+        err1_v = err1.rearrange("(G p t) k -> G p t k", p=P, t=4)
+        err2_v = err2.rearrange("(G p t) k -> G p t k", p=P, t=4)
+        x_v = x.rearrange("(G p t) f -> G p t f", p=P, t=4)
+
+        def load_e1(G, t0, n):
+            tl = kept("e1r_%d_%d" % (G, t0), [P, n, K1], BF16)
+            nc.sync.dma_start(out=tl[:], in_=err1_v[G][:, t0 : t0 + n, :])
+            for i in range(n):
+                e1_raw[(G, t0 + i)] = tl[:, i, :]
+
+        def load_e2(j):
+            G, t0 = j // 2, 2 * (j % 2)
+            tl = kept("e2r_%d" % j, [P, 2, K2], BF16)
+            nc.sync.dma_start(out=tl[:], in_=err2_v[G][:, t0 : t0 + 2, :])
+            e2_raw[j] = tl
+
+        def load_x(g, G):
+            name = "xr_%d" % G if g == 0 else "e1r_%d_2" % G
+            tl = kept(name, [P, 4, PASS], BF16)
+            nc.sync.dma_start(out=tl[:], in_=x_v[G][:, :, PASS * g : PASS * (g + 1)])
+            x_raw[(g, G)] = tl
+
+        def load_w2(g):
+            tl = kept("w2r_%d" % g, [P, 4, K2], BF16)
+            nc.sync.dma_start(out=tl[:], in_=w2[PASS * g : PASS * (g + 1), :].rearrange("(j p) k -> p j k", p=P))
+            w2_raw[g] = tl
+
+        def load_sw(rt):
+            tl = kept("swr_%d" % rt, [P, T], BF16)
+            nc.sync.dma_start(out=tl[:], in_=sample_w[P * rt : P * (rt + 1), :])
+            sw_raw[rt] = tl
+
+        def load_v(g):
+            tl = kept("vw_%d" % g, [P, 2, 2 * PASS], U8)
+            src = v_words.rearrange("k p n -> p k n")[:, :, 2 * PASS * g : 2 * PASS * (g + 1)]
+            nc.sync.dma_start(out=tl[:].bitcast(I32), in_=src.bitcast(I32))
+            v_w[g] = tl
+
+        def load_v_scales():
+            src = v_scales.rearrange("k q n -> q k n")
+            for Q in range(4):
+                nc.sync.dma_start(
+                    out=v_sc[32 * Q : 32 * Q + 4, :, :].bitcast(I32), in_=src[4 * Q : 4 * Q + 4, :, :].bitcast(I32)
+                )
+
+        al_col = kept("al_col", [P, 2, 4], BF16)
+        reg_col = kept("reg_col", [P, 2, 4], BF16)
+
+        load_e1(0, 0, 1)
+        load_e1(0, 1, 1)
+        load_v(0)
+        load_v_scales()
+        load_w2(0)
+        load_e2(0)
+        load_e1(0, 2, 2)
+        nc.sync.dma_start(out=al_col[:], in_=alpha.rearrange("(g p c) -> p g c", g=2, c=4))
+        load_e2(1)
+        load_x(0, 0)
+        for G in range(1, 4):
+            load_e1(G, 0, 2)
+            load_e2(2 * G)
+            load_x(0, G)
+            load_e1(G, 2, 2)
+            load_e2(2 * G + 1)
+        load_w2(1)
+        load_v(1)
+        nc.sync.dma_start(out=reg_col[:], in_=reg.rearrange("(g p c) -> p g c", g=2, c=4))
+        load_sw(0)
+        load_sw(1)
+        load_sw(2)
+        load_sw(3)
+
+        def turn(key, sources, dst):
+            bank = take_bank(key, [P, 2, 2, P])
+            for i, src in enumerate(sources):
+                words = src.bitcast(F32)
+                for u in range(2):
+                    nc.tensor.transpose(bank[:, i, u, :], words[:, u : 2 * P : 2], ident[:])
+            nc.scalar.copy(
+                out=dst.bitcast(F32).rearrange("p (i r u) -> p i r u", i=2, u=2),
+                in_=bank[:].rearrange("p i u r -> p i r u"),
+            )
+            give_bank(key)
+
+        def quantise(codes, scales, src):
+            nc.vector.quantize_mx(out=codes.bitcast(FP8X4), scales=scales, in_=src)
+
+        e1_q, e2_q, w2_q, sw_q, h_q = {}, {}, {}, {}, {}
+        pending = {}
+
+        def planes(name, cols):
+            return kept(name + "_c", [P, cols], U32), kept(name + "_s", [P, cols], U8)
+
+        def turn_e1(j, i):
+            G, t0 = j // 2, 2 * (j % 2)
+            if i == 0:
+                pending[("e1", j)] = stage.tile([P, 2048], BF16, tag="e1b", name="e1b", align_bytes=64)
+                e1_q[j] = planes("e1q%d" % j, 512)
+            raw = e1_raw[(G, t0 + i)]
+            turn("t", [raw[:, 0:PASS], raw[:, PASS : 2 * PASS]], pending[("e1", j)][:, 1024 * i : 1024 * (i + 1)])
+
+        def quant_e1(j):
+            quantise(e1_q[j][0][:], e1_q[j][1][:], pending.pop(("e1", j))[:])
+
+        def quant_e1_half(j, i):
+            c = slice(256 * i, 256 * (i + 1))
+            quantise(e1_q[j][0][:, c], e1_q[j][1][:, c], pending[("e1", j)][:, 1024 * i : 1024 * (i + 1)])
+
+        def turn_e2(j):
+            pending[("e2", j)] = stage.tile([P, 1024], BF16, tag="e2b", name="e2b", align_bytes=64)
+            e2_q[j] = planes("e2q%d" % j, 256)
+            turn("t", [e2_raw[j][:, 0, :], e2_raw[j][:, 1, :]], pending[("e2", j)][:])
+
+        def quant_e2(j):
+            quantise(e2_q[j][0][:], e2_q[j][1][:], pending.pop(("e2", j))[:])
+
+        def turn_w2(g, h):
+            if h == 0:
+                pending[("w2", g)] = stage.tile([P, 2048], BF16, tag="e1b", name="e1b", align_bytes=64)
+                w2_q[g] = planes("w2q%d" % g, 512)
+            turn("t", [w2_raw[g][:, 2 * h, :], w2_raw[g][:, 2 * h + 1, :]], pending[("w2", g)][:, 1024 * h : 1024 * (h + 1)])
+
+        def quant_w2(g):
+            quantise(w2_q[g][0][:], w2_q[g][1][:], pending.pop(("w2", g))[:])
+
+        def turn_sw(rt):
+            pending[("sw", rt)] = stage.tile([P, 2048], BF16, tag="e1b", name="e1b", align_bytes=64)
+            sw_q[rt] = planes("swq%d" % rt, 512)
+            for h in range(2):
+                srcs = [sw_raw[rt][:, PASS * G : PASS * (G + 1)] for G in (2 * h, 2 * h + 1)]
+                turn("t", srcs, pending[("sw", rt)][:, 1024 * h : 1024 * (h + 1)])
+
+        def quant_sw(rt):
+            quantise(sw_q[rt][0][:], sw_q[rt][1][:], pending.pop(("sw", rt))[:])
+
+        alpha_row = kept("alpha_row", [P, F], BF16)
+        bias_row = kept("bias_row", [P, F], F32)
+        bias_col = kept("bias_col", [P, 2, 4], F32)
+
+        def spread_alpha():
+            bank = take_bank("t", [P, 2, 2, P])
+            words = al_col[:].bitcast(F32)
+            for g in range(2):
+                for w in range(2):
+                    nc.tensor.transpose(bank[:, g, w, :], words[:, g, w : w + 1].to_broadcast([P, P]), ident[:])
+            nc.scalar.copy(
+                out=alpha_row[:].bitcast(F32).rearrange("p (g n w) -> p g n w", g=2, w=2),
+                in_=bank[:].rearrange("p g w n -> p g n w"),
+            )
+            give_bank("t")
+
+        def spread_bias(g):
+            bank = take_bank("t", [P, 4, P])
+            for c in range(4):
+                nc.tensor.transpose(bank[:, c, :], bias_col[:, g, c : c + 1].to_broadcast([P, P]), ident[:])
+            nc.scalar.copy(
+                out=bias_row[:, PASS * g : PASS * (g + 1)].rearrange("p (n c) -> p n c", c=4),
+                in_=bank[:].rearrange("p c n -> p n c"),
+            )
+            give_bank("t")
+
+        def mm1(s, i, passes):
+            g, j = s // 8, s % 8
+            if passes[0] == 0:
+                take_bank(("s1", s, i), [P, PASS])
+            acc = bank_of[("s1", s, i)][1]
+            cols = slice(PASS * g, PASS * (g + 1))
+            for kp in passes:
+                if kp < 2:
+                    c = slice(256 * i + P * kp, 256 * i + P * (kp + 1))
+                    lc, ls = e1_q[j][0][:, c], e1_q[j][1][:, c]
+                    rc, rs = v_w[g][:, kp, :].bitcast(FP4X4), v_sc[:, kp, cols]
+                else:
+                    c = slice(P * i, P * (i + 1))
+                    lc, ls = e2_q[j][0][:, c], e2_q[j][1][:, c]
+                    rc, rs = w2_q[g][0][:].bitcast(FP8X4), w2_q[g][1][:]
+                nc.tensor.matmul_mx(
+                    out=acc[:], lhsT=lc.bitcast(FP8X4), lhsT_scale=ls, rhs=rc, rhs_scale=rs, start=(kp == 0), stop=(kp == 2)
+                )
+
+        masks_of, h_rows, h_words = {}, {}, {}
+
+        def mask(s):
+            g, j = s // 8, s % 8
+            G, t0 = j // 2, 2 * (j % 2)
+            m = x_raw[(g, G)][:, t0 : t0 + 2, :]
+            masks_of[s] = m
+            nc.vector.tensor_tensor(
+                out=m,
+                in0=m,
+                in1=alpha_row[:, PASS * g : PASS * (g + 1)].unsqueeze(1).to_broadcast([P, 2, PASS]),
+                op=ALU.is_ge,
+            )
+
+        def apply_mask(s, i):
+            hh, t = s // 2, 2 * (s % 2) + i
+            if t == 0:
+                h_rows[hh] = stage.tile([P, 4, PASS], BF16, tag="h_rows", name="h_rows", bufs=2)
+            acc = bank_of[("s1", s, i)][1]
+            nc.vector.tensor_tensor(out=h_rows[hh][:, t, :], in0=acc[:], in1=masks_of[s][:, i, :], op=ALU.mult)
+            give_bank(("s1", s, i))
+
+        def interleave(hh, c0, c1, eng):
+            if c0 == 0:
+                h_words[hh] = stage.tile([P, 4 * PASS], BF16, tag="h_words", name="h_words", bufs=2, align_bytes=64)
+                h_q[hh] = planes("hq%d" % hh, PASS)
+            dst = h_words[hh][:, 4 * c0 : 4 * c1].rearrange("p (c i t) -> p c t i", i=4, t=4)
+            src = h_rows[hh][:, :, c0:c1].rearrange("p t (c i) -> p c t i", i=4)
+            if eng == "S":
+                nc.scalar.copy(out=dst, in_=src)
+            else:
+                nc.vector.tensor_copy(out=dst, in_=src)
+
+        def quant_h(hh, c0, c1):
+            quantise(h_q[hh][0][:, c0:c1], h_q[hh][1][:, c0:c1], h_words[hh][:, 4 * c0 : 4 * c1])
+
+        def mm2(g, rt, Gs):
+            if Gs[0] == 0:
+                take_bank(("s2", g, rt), [P, PASS])
+            acc = bank_of[("s2", g, rt)][1]
+            for G in Gs:
+                c = slice(P * G, P * (G + 1))
+                hq = h_q[4 * g + G]
+                nc.tensor.matmul_mx(
+                    out=acc[:], lhsT=sw_q[rt][0][:, c].bitcast(FP8X4), lhsT_scale=sw_q[rt][1][:, c],
+                    rhs=hq[0][:].bitcast(FP8X4), rhs_scale=hq[1][:], start=(G == 0), stop=(G == 3),
+                )
+
+        y_f32, y_bf, y_turned, y_q = {}, {}, {}, {}
+
+        def finish_y(g, rt):
+            acc = bank_of[("s2", g, rt)][1]
+            y = stage.tile([P, PASS], F32, tag="y", name="y", bufs=4)
+            nc.vector.tensor_tensor(out=y[:], in0=acc[:], in1=bias_row[:, PASS * g : PASS * (g + 1)], op=ALU.add)
+            give_bank(("s2", g, rt))
+            nc.sync.dma_start(out=out_0[P * rt : P * (rt + 1), PASS * g : PASS * (g + 1)], in_=y[:])
+            y_f32[(g, rt)] = y
+
+        def round_y(g, rt):
+            y = y_f32[(g, rt)]
+            yb = stage.tile([P, 2, P, 2], BF16, tag="y_bf", name="y_bf", bufs=4)
+            y_bf[(g, rt)] = yb
+            nc.scalar.copy(out=yb[:], in_=y[:].rearrange("r (p u e) -> r u p e", u=2, e=2))
+
+        def round_y_from_psum(g, rt):
+            acc = bank_of[("s2", g, rt)][1]
+            yb = stage.tile([P, 2, P, 2], BF16, tag="y_bf", name="y_bf", bufs=4)
+            y_bf[(g, rt)] = yb
+            order = "r (p u e) -> r u p e"
+            nc.vector.tensor_tensor(
+                out=yb[:], in0=acc[:].rearrange(order, u=2, e=2),
+                in1=bias_row[:, PASS * g : PASS * (g + 1)].rearrange(order, u=2, e=2), op=ALU.add,
+            )
+
+        def turn_y(g, rts, eng):
+            n = len(rts)
+            if rts[0] == 0:
+                y_turned[g] = stage.tile([P, 2048], BF16, tag="y_turned", name="y_turned", bufs=1, align_bytes=64)
+                y_q[g] = planes("yq%d" % g, R)
+            bank = take_bank("t", [P, n, 2, P])
+            for i in range(n):
+                words = y_bf[(g, rts[i])][:].rearrange("r u p e -> r u (p e)").bitcast(F32)
+                for u in range(2):
+                    nc.tensor.transpose(bank[:, i, u, :], words[:, u, :], ident[:])
+            dst = y_turned[g][:, PASS * rts[0] : PASS * (rts[-1] + 1)].bitcast(F32).rearrange("p (i r u) -> p i r u", i=n, u=2)
+            src = bank[:].rearrange("p i u r -> p i r u")
+            if eng == "S":
+                nc.scalar.copy(out=dst, in_=src)
+            else:
+                nc.vector.tensor_copy(out=dst, in_=src)
+            give_bank("t")
+
+        def quant_y(g, rts):
+            c = slice(P * rts[0], P * (rts[-1] + 1))
+            quantise(y_q[g][0][:, c], y_q[g][1][:, c], y_turned[g][:, PASS * rts[0] : PASS * (rts[-1] + 1)])
+
+        def store_words(g, rts):
+            c = slice(P * rts[0], P * (rts[-1] + 1))
+            dst = out_1[g].rearrange("p m t -> p (m t)").bitcast(I32)
+            nc.sync.dma_start(out=dst[:, c], in_=y_q[g][0][:, c].bitcast(I32))
+
+        def store_scales(g):
+            for Q in range(4):
+                eng = nc.sync if (g == 0 or Q % 2 == 0) else nc.scalar
+                eng.dma_start(
+                    out=out_2[g][4 * Q : 4 * Q + 4, :].bitcast(I32), in_=y_q[g][1][32 * Q : 32 * Q + 4, :].bitcast(I32)
+                )
+
+        turn_e1(0, 0)
+        turn_e1(0, 1)
+        quant_e1_half(0, 0)
+        quant_e1_half(0, 1)
+        mm1(0, 0, [0, 1])
+        mm1(0, 1, [0, 1])
+        turn_w2(0, 0)
+        turn_w2(0, 1)
+        turn_e2(0)
+        quant_w2(0)
+        quant_e2(0)
+        spread_alpha()
+
+        next_mask = [0]
+
+        def masks_to(n):
+            while next_mask[0] <= min(n, 15):
+                mask(next_mask[0])
+                next_mask[0] = next_mask[0] + 1
+
+        def half(n):
+            return n // 2, 256 * (n % 2), 256 * (n % 2 + 1)
+
+        for s in range(11):
+            if s > 0:
+                apply_mask(s - 1, 1)
+                masks_to(MASK_AHEAD[s])
+            if s >= 3:
+                quant_h(*half(s - 3))
+            if s < 7:
+                turn_e1(s + 1, 0)
+                turn_e1(s + 1, 1)
+                turn_e2(s + 1)
+                if s == 0:
+                    masks_to(0)
+                if s % 2 == 0:
+                    load_x(1, s // 2)
+                quant_e1(s + 1)
+                quant_e2(s + 1)
+            elif s == 7:
+                turn_w2(1, 0)
+                turn_w2(1, 1)
+                quant_w2(1)
+                nc.vector.tensor_tensor(out=bias_col[:], in0=reg_col[:], in1=al_col[:], op=ALU.mult)
+                turn_sw(0)
+                quant_sw(0)
+            else:
+                turn_sw(s - 7)
+                if s < 10:
+                    spread_bias(s - 8)
+                quant_sw(s - 7)
+            if s >= 2:
+                interleave(*half(s - 2), "S")
+            first = [2] if s == 0 else [0, 1, 2]
+            mm1(s, 0, first)
+            mm1(s, 1, first)
+            apply_mask(s, 0)
+
+        for s in range(11, 16):
+            apply_mask(s - 1, 1)
+            interleave(*half(s - 2), "S")
+            if s >= 12:
+                finish_y(0, s - 12)
+                round_y(0, s - 12)
+            masks_to(MASK_AHEAD[s])
+            quant_h(*half(s - 3))
+            if s == 15:
+                quant_y(0, [0, 1])
+                store_words(0, [0, 1])
+            mm1(s, 0, [0, 1, 2])
+            mm1(s, 1, [0, 1, 2])
+            if s <= 14:
+                mm2(0, s - 11, [0, 1, 2, 3])
+            if s == 14:
+                turn_y(0, [0, 1], "S")
+            apply_mask(s, 0)
+
+        for rt in range(3):
+            mm2(1, rt, [0, 1])
+        apply_mask(15, 1)
+        interleave(7, 0, 192, "S")
+        interleave(7, 192, 512, "V")
+        quant_h(*half(13))
+        turn_y(0, [2, 3], "S")
+        for rt in range(2):
+            mm2(1, rt, [2])
+        quant_h(7, 0, 512)
+        for rt in range(2):
+            mm2(1, rt, [3])
+        mm2(1, 2, [2, 3])
+        mm2(1, 3, [0, 1, 2, 3])
+        quant_y(0, [2, 3])
+        store_words(0, [2, 3])
+        store_scales(0)
+        for rt in range(3):
+            finish_y(1, rt)
+            round_y(1, rt)
+        round_y_from_psum(1, 3)
+        finish_y(1, 3)
+        turn_y(1, [0, 1], "S")
+        turn_y(1, [2, 3], "S")
+        quant_y(1, [0, 1])
+        store_words(1, [0, 1])
+        quant_y(1, [2, 3])
+        store_words(1, [2, 3])
+        store_scales(1)

@@ -18,6 +18,8 @@ ALU = mybir.AluOpType
 P = 128
 PASS = 512
 BANKS = 8
+SORTS = {2:[("e2",4,"S")],3:[("e2",5,"S")],4:[("e2",6,"S")],5:[("e2",7,"S")]}
+SORT_BUFS = 6
 MASK_AHEAD = [s + (1 if s >= 9 else 0) + (1 if s >= 11 else 0) for s in range(16)]
 
 
@@ -48,8 +50,9 @@ def tile_pact_threshold_gradient_k6_kernel(
 
         ident = kept("ident", [P, P], F32)
         make_identity(nc, ident[:])
-        v_sc = kept("v_sc", [P, 2, F], U8)
-        nc.vector.memset(v_sc[:].rearrange("p k n -> p (k n)").bitcast(I32), 0)
+        v_sc = [kept("v_sc%d" % g, [P, 2, PASS], U8) for g in range(2)]
+        for g in range(2):
+            nc.vector.memset(v_sc[g][:].rearrange("p k n -> p (k n)").bitcast(I32), 0)
 
         e1_raw, e2_raw, x_raw, sw_raw, w2_raw, v_w = {}, {}, {}, {}, {}, {}
         err1_v = err1.rearrange("(G p t) k -> G p t k", p=P, t=4)
@@ -90,48 +93,62 @@ def tile_pact_threshold_gradient_k6_kernel(
             nc.sync.dma_start(out=tl[:].bitcast(I32), in_=src.bitcast(I32))
             v_w[g] = tl
 
-        def load_v_scales():
-            src = v_scales.rearrange("k q n -> q k n")
+        def load_v_scales(g):
+            src = v_scales.rearrange("k q n -> q k n")[:, :, PASS * g : PASS * (g + 1)]
             for Q in range(4):
                 nc.sync.dma_start(
-                    out=v_sc[32 * Q : 32 * Q + 4, :, :].bitcast(I32), in_=src[4 * Q : 4 * Q + 4, :, :].bitcast(I32)
+                    out=v_sc[g][32 * Q : 32 * Q + 4, :, :].bitcast(I32), in_=src[4 * Q : 4 * Q + 4, :, :].bitcast(I32)
                 )
 
-        al_col = kept("al_col", [P, 2, 4], BF16)
-        reg_col = kept("reg_col", [P, 2, 4], BF16)
+        al_col = kept("al_col", [P, 8], BF16)
+        reg_col = kept("reg_col", [P, 8], BF16)
 
+        nc.sync.dma_start(out=al_col[:], in_=alpha.rearrange("(p c) -> p c", c=8))
         load_e1(0, 0, 1)
         load_e1(0, 1, 1)
+        load_v_scales(0)
         load_v(0)
-        load_v_scales()
+        load_e1(0, 2, 2)
         load_w2(0)
         load_e2(0)
-        load_e1(0, 2, 2)
-        nc.sync.dma_start(out=al_col[:], in_=alpha.rearrange("(g p c) -> p g c", g=2, c=4))
         load_e2(1)
-        load_x(0, 0)
         for G in range(1, 4):
             load_e1(G, 0, 2)
             load_e2(2 * G)
+            if G == 1:
+                load_x(0, 0)
             load_x(0, G)
             load_e1(G, 2, 2)
             load_e2(2 * G + 1)
         load_w2(1)
         load_v(1)
-        nc.sync.dma_start(out=reg_col[:], in_=reg.rearrange("(g p c) -> p g c", g=2, c=4))
+        load_v_scales(1)
+        nc.sync.dma_start(out=reg_col[:], in_=reg.rearrange("(p c) -> p c", c=8))
         load_sw(0)
         load_sw(1)
         load_sw(2)
         load_sw(3)
 
-        def turn(key, sources, dst):
-            bank = take_bank(key, [P, 2, 2, P])
+        def sort_words(src, n, eng):
+            dst = stage.tile([P, n * PASS], BF16, tag="sorted", name="sorted", bufs=SORT_BUFS)
+            a = dst[:].bitcast(F32).rearrange("r (i u p) -> r i u p", i=n, u=2)
+            b = src.bitcast(F32).rearrange("r (i p u) -> r i u p", i=n, u=2)
+            if eng == "S":
+                nc.scalar.copy(out=a, in_=b)
+            else:
+                nc.vector.tensor_copy(out=a, in_=b)
+            return dst
+
+        def turn(key, sources, dst, is_sorted=False):
+            n = len(sources)
+            bank = take_bank(key, [P, n, 2, P])
             for i, src in enumerate(sources):
                 words = src.bitcast(F32)
                 for u in range(2):
-                    nc.tensor.transpose(bank[:, i, u, :], words[:, u : 2 * P : 2], ident[:])
+                    part = words[:, P * u : P * (u + 1)] if is_sorted else words[:, u : 2 * P : 2]
+                    nc.tensor.transpose(bank[:, i, u, :], part, ident[:])
             nc.scalar.copy(
-                out=dst.bitcast(F32).rearrange("p (i r u) -> p i r u", i=2, u=2),
+                out=dst.bitcast(F32).rearrange("p (i r u) -> p i r u", i=n, u=2),
                 in_=bank[:].rearrange("p i u r -> p i r u"),
             )
             give_bank(key)
@@ -140,7 +157,7 @@ def tile_pact_threshold_gradient_k6_kernel(
             nc.vector.quantize_mx(out=codes.bitcast(FP8X4), scales=scales, in_=src)
 
         e1_q, e2_q, w2_q, sw_q, h_q = {}, {}, {}, {}, {}
-        pending = {}
+        pending, sorted_of = {}, {}
 
         def planes(name, cols):
             return kept(name + "_c", [P, cols], U32), kept(name + "_s", [P, cols], U8)
@@ -151,7 +168,10 @@ def tile_pact_threshold_gradient_k6_kernel(
                 pending[("e1", j)] = stage.tile([P, 2048], BF16, tag="e1b", name="e1b", align_bytes=64)
                 e1_q[j] = planes("e1q%d" % j, 512)
             raw = e1_raw[(G, t0 + i)]
-            turn("t", [raw[:, 0:PASS], raw[:, PASS : 2 * PASS]], pending[("e1", j)][:, 1024 * i : 1024 * (i + 1)])
+            st = sorted_of.get(("e1", j, i))
+            if st is not None:
+                raw = st
+            turn("t", [raw[:, 0:PASS], raw[:, PASS : 2 * PASS]], pending[("e1", j)][:, 1024 * i : 1024 * (i + 1)], st is not None)
 
         def quant_e1(j):
             quantise(e1_q[j][0][:], e1_q[j][1][:], pending.pop(("e1", j))[:])
@@ -163,7 +183,23 @@ def tile_pact_threshold_gradient_k6_kernel(
         def turn_e2(j):
             pending[("e2", j)] = stage.tile([P, 1024], BF16, tag="e2b", name="e2b", align_bytes=64)
             e2_q[j] = planes("e2q%d" % j, 256)
-            turn("t", [e2_raw[j][:, 0, :], e2_raw[j][:, 1, :]], pending[("e2", j)][:])
+            if ("e2", j) in sorted_of:
+                st = sorted_of[("e2", j)]
+                turn("t", [st[:, 0:PASS], st[:, PASS : 2 * PASS]], pending[("e2", j)][:], True)
+            else:
+                turn("t", [e2_raw[j][:, 0, :], e2_raw[j][:, 1, :]], pending[("e2", j)][:])
+
+        def sort_e2(j, eng):
+            sorted_of[("e2", j)] = sort_words(e2_raw[j][:].rearrange("p t k -> p (t k)"), 2, eng)
+
+        def sort_w2(g, h, eng):
+            sorted_of[("w2", g, h)] = sort_words(w2_raw[g][:, 2 * h : 2 * h + 2, :].rearrange("p j k -> p (j k)"), 2, eng)
+
+        def sort_sw(rt, h, eng):
+            sorted_of[("sw", rt, h)] = sort_words(sw_raw[rt][:, 1024 * h : 1024 * (h + 1)], 2, eng)
+
+        def sort_e1(j, i, eng):
+            sorted_of[("e1", j, i)] = sort_words(e1_raw[(j // 2, 2 * (j % 2) + i)], 2, eng)
 
         def quant_e2(j):
             quantise(e2_q[j][0][:], e2_q[j][1][:], pending.pop(("e2", j))[:])
@@ -172,7 +208,11 @@ def tile_pact_threshold_gradient_k6_kernel(
             if h == 0:
                 pending[("w2", g)] = stage.tile([P, 2048], BF16, tag="e1b", name="e1b", align_bytes=64)
                 w2_q[g] = planes("w2q%d" % g, 512)
-            turn("t", [w2_raw[g][:, 2 * h, :], w2_raw[g][:, 2 * h + 1, :]], pending[("w2", g)][:, 1024 * h : 1024 * (h + 1)])
+            srcs = [w2_raw[g][:, 2 * h, :], w2_raw[g][:, 2 * h + 1, :]]
+            st = sorted_of.get(("w2", g, h))
+            if st is not None:
+                srcs = [st[:, 0:PASS], st[:, PASS : 2 * PASS]]
+            turn("t", srcs, pending[("w2", g)][:, 1024 * h : 1024 * (h + 1)], st is not None)
 
         def quant_w2(g):
             quantise(w2_q[g][0][:], w2_q[g][1][:], pending.pop(("w2", g))[:])
@@ -182,33 +222,37 @@ def tile_pact_threshold_gradient_k6_kernel(
             sw_q[rt] = planes("swq%d" % rt, 512)
             for h in range(2):
                 srcs = [sw_raw[rt][:, PASS * G : PASS * (G + 1)] for G in (2 * h, 2 * h + 1)]
-                turn("t", srcs, pending[("sw", rt)][:, 1024 * h : 1024 * (h + 1)])
+                st = sorted_of.get(("sw", rt, h))
+                if st is not None:
+                    srcs = [st[:, 0:PASS], st[:, PASS : 2 * PASS]]
+                turn("t", srcs, pending[("sw", rt)][:, 1024 * h : 1024 * (h + 1)], st is not None)
 
         def quant_sw(rt):
             quantise(sw_q[rt][0][:], sw_q[rt][1][:], pending.pop(("sw", rt))[:])
 
         alpha_row = kept("alpha_row", [P, F], BF16)
         bias_row = kept("bias_row", [P, F], F32)
-        bias_col = kept("bias_col", [P, 2, 4], F32)
+        bias_col = kept("bias_col", [P, 8], F32)
 
         def spread_alpha():
-            bank = take_bank("t", [P, 2, 2, P])
+            bank = take_bank("alpha", [P, 4, P])
             words = al_col[:].bitcast(F32)
-            for g in range(2):
-                for w in range(2):
-                    nc.tensor.transpose(bank[:, g, w, :], words[:, g, w : w + 1].to_broadcast([P, P]), ident[:])
-            nc.scalar.copy(
-                out=alpha_row[:].bitcast(F32).rearrange("p (g n w) -> p g n w", g=2, w=2),
-                in_=bank[:].rearrange("p g w n -> p g n w"),
+            for w in range(4):
+                nc.tensor.transpose(bank[:, w, :], words[:, w : w + 1].to_broadcast([P, P]), ident[:])
+
+        def copy_alpha():
+            nc.vector.tensor_copy(
+                out=alpha_row[:].bitcast(F32).rearrange("p (n w) -> p n w", w=4),
+                in_=bank_of["alpha"][1][:].rearrange("p w n -> p n w"),
             )
-            give_bank("t")
+            give_bank("alpha")
 
         def spread_bias(g):
             bank = take_bank("t", [P, 4, P])
             for c in range(4):
-                nc.tensor.transpose(bank[:, c, :], bias_col[:, g, c : c + 1].to_broadcast([P, P]), ident[:])
+                nc.tensor.transpose(bank[:, c, :], bias_col[:, 4 * g + c : 4 * g + c + 1].to_broadcast([P, P]), ident[:])
             nc.scalar.copy(
-                out=bias_row[:, PASS * g : PASS * (g + 1)].rearrange("p (n c) -> p n c", c=4),
+                out=bias_row[:].rearrange("p (n c) -> p n c", c=8)[:, :, 4 * g : 4 * g + 4],
                 in_=bank[:].rearrange("p c n -> p n c"),
             )
             give_bank("t")
@@ -218,12 +262,11 @@ def tile_pact_threshold_gradient_k6_kernel(
             if passes[0] == 0:
                 take_bank(("s1", s, i), [P, PASS])
             acc = bank_of[("s1", s, i)][1]
-            cols = slice(PASS * g, PASS * (g + 1))
             for kp in passes:
                 if kp < 2:
                     c = slice(256 * i + P * kp, 256 * i + P * (kp + 1))
                     lc, ls = e1_q[j][0][:, c], e1_q[j][1][:, c]
-                    rc, rs = v_w[g][:, kp, :].bitcast(FP4X4), v_sc[:, kp, cols]
+                    rc, rs = v_w[g][:, kp, :].bitcast(FP4X4), v_sc[g][:, kp, :]
                 else:
                     c = slice(P * i, P * (i + 1))
                     lc, ls = e2_q[j][0][:, c], e2_q[j][1][:, c]
@@ -340,20 +383,58 @@ def tile_pact_threshold_gradient_k6_kernel(
                     out=out_2[g][4 * Q : 4 * Q + 4, :].bitcast(I32), in_=y_q[g][1][32 * Q : 32 * Q + 4, :].bitcast(I32)
                 )
 
-        turn_e1(0, 0)
-        turn_e1(0, 1)
-        quant_e1_half(0, 0)
-        quant_e1_half(0, 1)
+        e1_q[0] = planes("e1q0", 512)
+        first_bf = [stage.tile([P, PASS], BF16, tag="first_bf", name="first_bf", bufs=4, align_bytes=64) for n in range(4)]
+
+        def first_piece(src, i, kp):
+            turn("t", [src], first_bf[2 * i + kp][:])
+            c = slice(256 * i + P * kp, 256 * i + P * (kp + 1))
+            quantise(e1_q[0][0][:, c], e1_q[0][1][:, c], first_bf[2 * i + kp][:])
+
+        spread_alpha()
+        copy_alpha()
+        for i in range(2):
+            for kp in range(2):
+                first_piece(e1_raw[(0, i)][:, PASS * kp : PASS * (kp + 1)], i, kp)
         mm1(0, 0, [0, 1])
         mm1(0, 1, [0, 1])
+        sort_e1(1, 0, "S")
+        sort_e1(1, 1, "S")
+        sort_w2(0, 0, "V")
+        sort_w2(0, 1, "V")
+        sort_e2(0, "V")
+        turn_e1(1, 0)
+        turn_e1(1, 1)
+        sort_e2(1, "V")
+        quant_e1_half(1, 0)
+        quant_e1_half(1, 1)
         turn_w2(0, 0)
         turn_w2(0, 1)
         turn_e2(0)
+        turn_e2(1)
+        mm1(1, 0, [0, 1])
+        mm1(1, 1, [0, 1])
+        sort_e2(2, "V")
         quant_w2(0)
         quant_e2(0)
-        spread_alpha()
+        mask(0)
+        quant_e2(1)
+        load_x(1, 0)
+        turn_e1(2, 0)
+        turn_e1(2, 1)
+        turn_e2(2)
+        mask(1)
+        for s in range(2):
+            for i in range(2):
+                mm1(s, i, [2])
+        apply_mask(0, 0)
+        quant_e1(2)
+        apply_mask(0, 1)
+        quant_e2(2)
+        apply_mask(1, 0)
 
-        next_mask = [0]
+        sorter = {"e2": sort_e2, "w2": sort_w2, "sw": sort_sw, "e1": sort_e1}
+        next_mask = [2]
 
         def masks_to(n):
             while next_mask[0] <= min(n, 15):
@@ -363,7 +444,7 @@ def tile_pact_threshold_gradient_k6_kernel(
         def half(n):
             return n // 2, 256 * (n % 2), 256 * (n % 2 + 1)
 
-        for s in range(11):
+        for s in range(2, 11):
             if s > 0:
                 apply_mask(s - 1, 1)
                 masks_to(MASK_AHEAD[s])
@@ -373,8 +454,6 @@ def tile_pact_threshold_gradient_k6_kernel(
                 turn_e1(s + 1, 0)
                 turn_e1(s + 1, 1)
                 turn_e2(s + 1)
-                if s == 0:
-                    masks_to(0)
                 if s % 2 == 0:
                     load_x(1, s // 2)
                 quant_e1(s + 1)
@@ -391,24 +470,32 @@ def tile_pact_threshold_gradient_k6_kernel(
                 if s < 10:
                     spread_bias(s - 8)
                 quant_sw(s - 7)
+            for item in SORTS.get(s, []):
+                sorter[item[0]](*item[1:])
             if s >= 2:
                 interleave(*half(s - 2), "S")
-            first = [2] if s == 0 else [0, 1, 2]
-            mm1(s, 0, first)
-            mm1(s, 1, first)
+            mm1(s, 0, [0, 1, 2])
+            mm1(s, 1, [0, 1, 2])
             apply_mask(s, 0)
 
         for s in range(11, 16):
             apply_mask(s - 1, 1)
-            interleave(*half(s - 2), "S")
+            if s == 11:
+                interleave(*half(s - 2), "S")
+            elif s % 2 == 0:
+                interleave((s - 2) // 2, 0, 256, "S")
             if s >= 12:
                 finish_y(0, s - 12)
                 round_y(0, s - 12)
             masks_to(MASK_AHEAD[s])
-            quant_h(*half(s - 3))
-            if s == 15:
-                quant_y(0, [0, 1])
-                store_words(0, [0, 1])
+            if s >= 12 and s % 2 == 0:
+                interleave((s - 2) // 2, 256, 512, "S")
+            if s <= 12:
+                quant_h(*half(s - 3))
+            elif s == 13:
+                quant_h(5, 0, 512)
+            elif s == 15:
+                quant_h(6, 0, 256)
             mm1(s, 0, [0, 1, 2])
             mm1(s, 1, [0, 1, 2])
             if s <= 14:
@@ -419,10 +506,10 @@ def tile_pact_threshold_gradient_k6_kernel(
 
         for rt in range(3):
             mm2(1, rt, [0, 1])
+        quant_h(6, 256, 512)
         apply_mask(15, 1)
-        interleave(7, 0, 192, "S")
-        interleave(7, 192, 512, "V")
-        quant_h(*half(13))
+        interleave(7, 0, 160, "S")
+        interleave(7, 160, 512, "V")
         turn_y(0, [2, 3], "S")
         for rt in range(2):
             mm2(1, rt, [2])
@@ -431,8 +518,9 @@ def tile_pact_threshold_gradient_k6_kernel(
             mm2(1, rt, [3])
         mm2(1, 2, [2, 3])
         mm2(1, 3, [0, 1, 2, 3])
+        quant_y(0, [0, 1])
         quant_y(0, [2, 3])
-        store_words(0, [2, 3])
+        store_words(0, [0, 1, 2, 3])
         store_scales(0)
         for rt in range(3):
             finish_y(1, rt)
@@ -440,7 +528,8 @@ def tile_pact_threshold_gradient_k6_kernel(
         round_y_from_psum(1, 3)
         finish_y(1, 3)
         turn_y(1, [0, 1], "S")
-        turn_y(1, [2, 3], "S")
+        turn_y(1, [3], "V")
+        turn_y(1, [2], "S")
         quant_y(1, [0, 1])
         store_words(1, [0, 1])
         quant_y(1, [2, 3])

@@ -17,10 +17,20 @@ ALU = mybir.AluOpType
 
 P = 128
 PASS = 512
+HALF = PASS // 2
+SLOTS = 4
+GROUPS = T // PASS
+PAIRS = 2 * GROUPS
+ROW_TILES = R // P
 BANKS = 8
-SORTS = {2:[("e2",4,"S")],3:[("e2",5,"S")],4:[("e2",6,"S")],5:[("e2",7,"S")]}
-SORT_BUFS = 6
-MASK_AHEAD = [s + (1 if s >= 9 else 0) + (1 if s >= 11 else 0) for s in range(16)]
+
+LAST_ERR_STEP = PAIRS - 2
+W2_STEP = PAIRS - 1
+STAGE2_STEP = W2_STEP + ROW_TILES
+LAST_STEP = 2 * PAIRS - 1
+SCALAR_EMPTIES = (1, STAGE2_STEP, STAGE2_STEP + 2)
+SCALAR_SORTS = (4, 6)
+TAIL_SCALAR_COLUMNS = 160
 
 
 def tile_pact_threshold_gradient_k6_kernel(
@@ -34,504 +44,491 @@ def tile_pact_threshold_gradient_k6_kernel(
         ctx.enter_context(tc.manual_schedule())
 
         free_banks = list(range(BANKS))
-        bank_of = {}
+        held = {}
 
         def take_bank(key, shape):
             b = free_banks.pop(0)
             bank = psum.tile(shape, F32, tag="bank%d" % b, name="bank%d" % b)
-            bank_of[key] = (b, bank)
+            held[key] = (b, bank)
             return bank
 
         def give_bank(key):
-            free_banks.append(bank_of.pop(key)[0])
+            free_banks.append(held.pop(key)[0])
 
         def kept(name, shape, dtype):
             return keep.tile(shape, dtype, name=name, tag=name, align_bytes=64)
 
+        def mx_tiles(name, columns):
+            return kept(name + "_c", [P, columns], U32), kept(name + "_s", [P, columns], U8)
+
+        scalar_copy, vector_copy = nc.scalar.copy, nc.vector.tensor_copy
+
+        def quantise(tiles, columns, src):
+            nc.vector.quantize_mx(out=tiles[0][:, columns].bitcast(FP8X4), scales=tiles[1][:, columns], in_=src)
+
         ident = kept("ident", [P, P], F32)
         make_identity(nc, ident[:])
-        v_sc = [kept("v_sc%d" % g, [P, 2, PASS], U8) for g in range(2)]
+        v_scale = [kept("v_sc%d" % g, [P, 2, PASS], U8) for g in range(2)]
         for g in range(2):
-            nc.vector.memset(v_sc[g][:].rearrange("p k n -> p (k n)").bitcast(I32), 0)
+            nc.vector.memset(v_scale[g][:].rearrange("p k n -> p (k n)").bitcast(I32), 0)
 
-        e1_raw, e2_raw, x_raw, sw_raw, w2_raw, v_w = {}, {}, {}, {}, {}, {}
-        err1_v = err1.rearrange("(G p t) k -> G p t k", p=P, t=4)
-        err2_v = err2.rearrange("(G p t) k -> G p t k", p=P, t=4)
-        x_v = x.rearrange("(G p t) f -> G p t f", p=P, t=4)
+        err1_raw, err2_raw, x_raw, sw_raw, w2_raw, v_code = {}, {}, {}, {}, {}, {}
+        err1_v = err1.rearrange("(G p t) k -> G p t k", p=P, t=SLOTS)
+        err2_v = err2.rearrange("(G p t) k -> G p t k", p=P, t=SLOTS)
+        x_v = x.rearrange("(G p t) f -> G p t f", p=P, t=SLOTS)
 
-        def load_e1(G, t0, n):
+        def load_err1(G, t0, n):
             tl = kept("e1r_%d_%d" % (G, t0), [P, n, K1], BF16)
             nc.sync.dma_start(out=tl[:], in_=err1_v[G][:, t0 : t0 + n, :])
             for i in range(n):
-                e1_raw[(G, t0 + i)] = tl[:, i, :]
+                err1_raw[(G, t0 + i)] = tl[:, i, :]
 
-        def load_e2(j):
-            G, t0 = j // 2, 2 * (j % 2)
-            tl = kept("e2r_%d" % j, [P, 2, K2], BF16)
-            nc.sync.dma_start(out=tl[:], in_=err2_v[G][:, t0 : t0 + 2, :])
-            e2_raw[j] = tl
+        def load_err2(j):
+            t0 = 2 * (j % 2)
+            err2_raw[j] = kept("e2r_%d" % j, [P, 2, K2], BF16)
+            nc.sync.dma_start(out=err2_raw[j][:], in_=err2_v[j // 2][:, t0 : t0 + 2, :])
 
         def load_x(g, G):
-            name = "xr_%d" % G if g == 0 else "e1r_%d_2" % G
-            tl = kept(name, [P, 4, PASS], BF16)
-            nc.sync.dma_start(out=tl[:], in_=x_v[G][:, :, PASS * g : PASS * (g + 1)])
-            x_raw[(g, G)] = tl
+            x_raw[(g, G)] = kept("xr_%d" % G if g == 0 else "e1r_%d_2" % G, [P, SLOTS, PASS], BF16)
+            nc.sync.dma_start(out=x_raw[(g, G)][:], in_=x_v[G][:, :, PASS * g : PASS * (g + 1)])
 
         def load_w2(g):
-            tl = kept("w2r_%d" % g, [P, 4, K2], BF16)
-            nc.sync.dma_start(out=tl[:], in_=w2[PASS * g : PASS * (g + 1), :].rearrange("(j p) k -> p j k", p=P))
-            w2_raw[g] = tl
+            w2_raw[g] = kept("w2r_%d" % g, [P, 4, K2], BF16)
+            nc.sync.dma_start(
+                out=w2_raw[g][:], in_=w2[PASS * g : PASS * (g + 1), :].rearrange("(p j) k -> p j k", p=P)
+            )
 
         def load_sw(rt):
-            tl = kept("swr_%d" % rt, [P, T], BF16)
-            nc.sync.dma_start(out=tl[:], in_=sample_w[P * rt : P * (rt + 1), :])
-            sw_raw[rt] = tl
+            sw_raw[rt] = kept("e1r_%d_0" % (rt + 1) if rt < 2 else "swr_%d" % rt, [P, T], BF16)
+            nc.sync.dma_start(out=sw_raw[rt][:], in_=sample_w[P * rt : P * (rt + 1), :])
 
         def load_v(g):
-            tl = kept("vw_%d" % g, [P, 2, 2 * PASS], U8)
+            v_code[g] = kept("vw_%d" % g, [P, 2, 2 * PASS], U8)
             src = v_words.rearrange("k p n -> p k n")[:, :, 2 * PASS * g : 2 * PASS * (g + 1)]
-            nc.sync.dma_start(out=tl[:].bitcast(I32), in_=src.bitcast(I32))
-            v_w[g] = tl
+            nc.sync.dma_start(out=v_code[g][:].bitcast(I32), in_=src.bitcast(I32))
 
         def load_v_scales(g):
             src = v_scales.rearrange("k q n -> q k n")[:, :, PASS * g : PASS * (g + 1)]
             for Q in range(4):
                 nc.sync.dma_start(
-                    out=v_sc[g][32 * Q : 32 * Q + 4, :, :].bitcast(I32), in_=src[4 * Q : 4 * Q + 4, :, :].bitcast(I32)
+                    out=v_scale[g][32 * Q : 32 * Q + 4, :, :].bitcast(I32),
+                    in_=src[4 * Q : 4 * Q + 4, :, :].bitcast(I32),
                 )
 
-        al_col = kept("al_col", [P, 8], BF16)
+        alpha_col = kept("al_col", [P, 8], BF16)
         reg_col = kept("reg_col", [P, 8], BF16)
 
-        nc.sync.dma_start(out=al_col[:], in_=alpha.rearrange("(p c) -> p c", c=8))
-        load_e1(0, 0, 1)
-        load_e1(0, 1, 1)
+        nc.sync.dma_start(out=alpha_col[:], in_=alpha.rearrange("(p c) -> p c", c=8))
+        load_err1(0, 0, 1)
+        load_err1(0, 1, 1)
         load_v_scales(0)
         load_v(0)
-        load_e1(0, 2, 2)
+        load_err1(0, 2, 2)
         load_w2(0)
-        load_e2(0)
-        load_e2(1)
-        for G in range(1, 4):
-            load_e1(G, 0, 2)
-            load_e2(2 * G)
+        load_err2(0)
+        load_err2(1)
+        for G in range(1, GROUPS):
+            load_err1(G, 0, 2)
             if G == 1:
                 load_x(0, 0)
+            load_err2(2 * G)
+            load_err1(G, 2, 2)
+            load_err2(2 * G + 1)
             load_x(0, G)
-            load_e1(G, 2, 2)
-            load_e2(2 * G + 1)
         load_w2(1)
         load_v(1)
         load_v_scales(1)
         nc.sync.dma_start(out=reg_col[:], in_=reg.rearrange("(p c) -> p c", c=8))
-        load_sw(0)
-        load_sw(1)
-        load_sw(2)
-        load_sw(3)
 
-        def sort_words(src, n, eng):
-            dst = stage.tile([P, n * PASS], BF16, tag="sorted", name="sorted", bufs=SORT_BUFS)
-            a = dst[:].bitcast(F32).rearrange("r (i u p) -> r i u p", i=n, u=2)
-            b = src.bitcast(F32).rearrange("r (i p u) -> r i u p", i=n, u=2)
-            if eng == "S":
-                nc.scalar.copy(out=a, in_=b)
-            else:
-                nc.vector.tensor_copy(out=a, in_=b)
-            return dst
+        err1_mx, err2_mx, w2_mx, sw_mx, h_mx, y_mx = {}, {}, {}, {}, {}, {}
+        turned, sorted_pairs = {}, {}
 
-        def turn(key, sources, dst, is_sorted=False):
-            n = len(sources)
-            bank = take_bank(key, [P, n, 2, P])
-            for i, src in enumerate(sources):
-                words = src.bitcast(F32)
+        def sort_pairs(key, src, copier):
+            dst = stage.tile([P, 2 * PASS], BF16, tag="sorted", name="sorted", bufs=4)
+            copier(
+                out=dst[:].bitcast(F32).rearrange("r (i u p) -> r i u p", i=2, u=2),
+                in_=src.bitcast(F32).rearrange("r (i p u) -> r i u p", i=2, u=2),
+            )
+            sorted_pairs[key] = dst
+
+        def transpose_runs(key, runs):
+            is_sorted = key in sorted_pairs
+            if is_sorted:
+                runs = [sorted_pairs[key][:, PASS * i : PASS * (i + 1)] for i in range(2)]
+            bank = take_bank("turn", [P, len(runs), 2, P])
+            for i, run in enumerate(runs):
+                pairs = run.bitcast(F32)
                 for u in range(2):
-                    part = words[:, P * u : P * (u + 1)] if is_sorted else words[:, u : 2 * P : 2]
+                    part = pairs[:, P * u : P * (u + 1)] if is_sorted else pairs[:, u : 2 * P : 2]
                     nc.tensor.transpose(bank[:, i, u, :], part, ident[:])
+            return bank
+
+        def turn(key, runs, dst):
+            bank = transpose_runs(key, runs)
             nc.scalar.copy(
-                out=dst.bitcast(F32).rearrange("p (i r u) -> p i r u", i=n, u=2),
+                out=dst.bitcast(F32).rearrange("p (i r u) -> p i r u", i=len(runs), u=2),
                 in_=bank[:].rearrange("p i u r -> p i r u"),
             )
-            give_bank(key)
+            give_bank("turn")
 
-        def quantise(codes, scales, src):
-            nc.vector.quantize_mx(out=codes.bitcast(FP8X4), scales=scales, in_=src)
+        def wide_tile():
+            return stage.tile([P, 4 * PASS], BF16, tag="wide", name="wide", align_bytes=64)
 
-        e1_q, e2_q, w2_q, sw_q, h_q = {}, {}, {}, {}, {}
-        pending, sorted_of = {}, {}
+        def err1_slot(j, i):
+            return err1_raw[(j // 2, 2 * (j % 2) + i)]
 
-        def planes(name, cols):
-            return kept(name + "_c", [P, cols], U32), kept(name + "_s", [P, cols], U8)
+        def turn_err1(j):
+            turned[("err1", j)] = wide_tile()
+            err1_mx[j] = mx_tiles("e1q%d" % j, PASS)
+            for i in range(2):
+                raw = err1_slot(j, i)
+                dst = turned[("err1", j)][:, 2 * PASS * i : 2 * PASS * (i + 1)]
+                turn(("err1", j, i), [raw[:, 0:PASS], raw[:, PASS : 2 * PASS]], dst)
 
-        def turn_e1(j, i):
-            G, t0 = j // 2, 2 * (j % 2)
-            if i == 0:
-                pending[("e1", j)] = stage.tile([P, 2048], BF16, tag="e1b", name="e1b", align_bytes=64)
-                e1_q[j] = planes("e1q%d" % j, 512)
-            raw = e1_raw[(G, t0 + i)]
-            st = sorted_of.get(("e1", j, i))
-            if st is not None:
-                raw = st
-            turn("t", [raw[:, 0:PASS], raw[:, PASS : 2 * PASS]], pending[("e1", j)][:, 1024 * i : 1024 * (i + 1)], st is not None)
+        def quantise_err1(j):
+            quantise(err1_mx[j], slice(0, PASS), turned[("err1", j)][:])
 
-        def quant_e1(j):
-            quantise(e1_q[j][0][:], e1_q[j][1][:], pending.pop(("e1", j))[:])
+        def turn_err2(j):
+            turned[("err2", j)] = stage.tile([P, 2 * PASS], BF16, tag="e2b", name="e2b", align_bytes=64)
+            err2_mx[j] = mx_tiles("e2q%d" % j, HALF)
+            turn(("err2", j), [err2_raw[j][:, 0, :], err2_raw[j][:, 1, :]], turned[("err2", j)][:])
 
-        def quant_e1_half(j, i):
-            c = slice(256 * i, 256 * (i + 1))
-            quantise(e1_q[j][0][:, c], e1_q[j][1][:, c], pending[("e1", j)][:, 1024 * i : 1024 * (i + 1)])
+        def sort_err2(j, copier):
+            sort_pairs(("err2", j), err2_raw[j][:].rearrange("p t k -> p (t k)"), copier)
 
-        def turn_e2(j):
-            pending[("e2", j)] = stage.tile([P, 1024], BF16, tag="e2b", name="e2b", align_bytes=64)
-            e2_q[j] = planes("e2q%d" % j, 256)
-            if ("e2", j) in sorted_of:
-                st = sorted_of[("e2", j)]
-                turn("t", [st[:, 0:PASS], st[:, PASS : 2 * PASS]], pending[("e2", j)][:], True)
-            else:
-                turn("t", [e2_raw[j][:, 0, :], e2_raw[j][:, 1, :]], pending[("e2", j)][:])
+        def quantise_err2(j):
+            quantise(err2_mx[j], slice(0, HALF), turned[("err2", j)][:])
 
-        def sort_e2(j, eng):
-            sorted_of[("e2", j)] = sort_words(e2_raw[j][:].rearrange("p t k -> p (t k)"), 2, eng)
+        def turn_w2(g):
+            turned[("w2", g)] = wide_tile()
+            w2_mx[g] = mx_tiles("w2q%d" % g, PASS)
+            by_channel = turned[("w2", g)][:].bitcast(F32).rearrange("p (r j u) -> p r j u", j=4, u=2)
+            for h in range(2):
+                bank = transpose_runs(("w2", g, h), [w2_raw[g][:, 2 * h, :], w2_raw[g][:, 2 * h + 1, :]])
+                nc.scalar.copy(out=by_channel[:, :, 2 * h : 2 * h + 2, :], in_=bank[:].rearrange("p j u r -> p r j u"))
+                give_bank("turn")
 
-        def sort_w2(g, h, eng):
-            sorted_of[("w2", g, h)] = sort_words(w2_raw[g][:, 2 * h : 2 * h + 2, :].rearrange("p j k -> p (j k)"), 2, eng)
-
-        def sort_sw(rt, h, eng):
-            sorted_of[("sw", rt, h)] = sort_words(sw_raw[rt][:, 1024 * h : 1024 * (h + 1)], 2, eng)
-
-        def sort_e1(j, i, eng):
-            sorted_of[("e1", j, i)] = sort_words(e1_raw[(j // 2, 2 * (j % 2) + i)], 2, eng)
-
-        def quant_e2(j):
-            quantise(e2_q[j][0][:], e2_q[j][1][:], pending.pop(("e2", j))[:])
-
-        def turn_w2(g, h):
-            if h == 0:
-                pending[("w2", g)] = stage.tile([P, 2048], BF16, tag="e1b", name="e1b", align_bytes=64)
-                w2_q[g] = planes("w2q%d" % g, 512)
-            srcs = [w2_raw[g][:, 2 * h, :], w2_raw[g][:, 2 * h + 1, :]]
-            st = sorted_of.get(("w2", g, h))
-            if st is not None:
-                srcs = [st[:, 0:PASS], st[:, PASS : 2 * PASS]]
-            turn("t", srcs, pending[("w2", g)][:, 1024 * h : 1024 * (h + 1)], st is not None)
-
-        def quant_w2(g):
-            quantise(w2_q[g][0][:], w2_q[g][1][:], pending.pop(("w2", g))[:])
+        def quantise_w2(g):
+            quantise(w2_mx[g], slice(0, PASS), turned[("w2", g)][:])
 
         def turn_sw(rt):
-            pending[("sw", rt)] = stage.tile([P, 2048], BF16, tag="e1b", name="e1b", align_bytes=64)
-            sw_q[rt] = planes("swq%d" % rt, 512)
+            turned[("sw", rt)] = wide_tile()
+            sw_mx[rt] = mx_tiles("swq%d" % rt, PASS)
             for h in range(2):
-                srcs = [sw_raw[rt][:, PASS * G : PASS * (G + 1)] for G in (2 * h, 2 * h + 1)]
-                st = sorted_of.get(("sw", rt, h))
-                if st is not None:
-                    srcs = [st[:, 0:PASS], st[:, PASS : 2 * PASS]]
-                turn("t", srcs, pending[("sw", rt)][:, 1024 * h : 1024 * (h + 1)], st is not None)
+                runs = [sw_raw[rt][:, PASS * G : PASS * (G + 1)] for G in (2 * h, 2 * h + 1)]
+                turn(("sw", rt, h), runs, turned[("sw", rt)][:, 2 * PASS * h : 2 * PASS * (h + 1)])
 
-        def quant_sw(rt):
-            quantise(sw_q[rt][0][:], sw_q[rt][1][:], pending.pop(("sw", rt))[:])
+        def quantise_sw(rt):
+            quantise(sw_mx[rt], slice(0, PASS), turned[("sw", rt)][:])
 
-        alpha_row = kept("alpha_row", [P, F], BF16)
+        alpha_row = kept("alpha_row", [P, 2, SLOTS, PASS], BF16)
         bias_row = kept("bias_row", [P, F], F32)
         bias_col = kept("bias_col", [P, 8], F32)
 
         def spread_alpha():
-            bank = take_bank("alpha", [P, 4, P])
-            words = al_col[:].bitcast(F32)
+            bank = take_bank("turn", [P, 4, P])
+            pairs = alpha_col[:].bitcast(F32)
             for w in range(4):
-                nc.tensor.transpose(bank[:, w, :], words[:, w : w + 1].to_broadcast([P, P]), ident[:])
-
-        def copy_alpha():
+                nc.tensor.transpose(bank[:, w, :], pairs[:, w : w + 1].to_broadcast([P, P]), ident[:])
             nc.vector.tensor_copy(
-                out=alpha_row[:].bitcast(F32).rearrange("p (n w) -> p n w", w=4),
-                in_=bank_of["alpha"][1][:].rearrange("p w n -> p n w"),
+                out=alpha_row[:, :, 0, :].bitcast(F32).rearrange("p g (n w) -> p g n w", w=4),
+                in_=bank[:].rearrange("p w (g n) -> p g n w", g=2),
             )
-            give_bank("alpha")
+            give_bank("turn")
 
-        def spread_bias(g):
-            bank = take_bank("t", [P, 4, P])
+        def repeat_alpha():
+            nc.vector.tensor_copy(
+                out=alpha_row[:, :, 1:SLOTS, :], in_=alpha_row[:, :, 0:1, :].to_broadcast([P, 2, SLOTS - 1, PASS])
+            )
+
+        def spread_bias(h):
+            bank = take_bank("turn", [P, 4, P])
             for c in range(4):
-                nc.tensor.transpose(bank[:, c, :], bias_col[:, 4 * g + c : 4 * g + c + 1].to_broadcast([P, P]), ident[:])
+                column = bias_col[:, 4 * h + c : 4 * h + c + 1]
+                nc.tensor.transpose(bank[:, c, :], column.to_broadcast([P, P]), ident[:])
             nc.scalar.copy(
-                out=bias_row[:].rearrange("p (n c) -> p n c", c=8)[:, :, 4 * g : 4 * g + 4],
+                out=bias_row[:].rearrange("p (n c) -> p n c", c=8)[:, :, 4 * h : 4 * h + 4],
                 in_=bank[:].rearrange("p c n -> p n c"),
             )
-            give_bank("t")
+            give_bank("turn")
 
-        def mm1(s, i, passes):
-            g, j = s // 8, s % 8
+        def stage1(s, i, passes):
+            g, j = s // PAIRS, s % PAIRS
             if passes[0] == 0:
-                take_bank(("s1", s, i), [P, PASS])
-            acc = bank_of[("s1", s, i)][1]
+                take_bank(("sums", s, i), [P, PASS])
+            acc = held[("sums", s, i)][1]
             for kp in passes:
                 if kp < 2:
-                    c = slice(256 * i + P * kp, 256 * i + P * (kp + 1))
-                    lc, ls = e1_q[j][0][:, c], e1_q[j][1][:, c]
-                    rc, rs = v_w[g][:, kp, :].bitcast(FP4X4), v_sc[g][:, kp, :]
+                    c = slice(HALF * i + P * kp, HALF * i + P * (kp + 1))
+                    left = err1_mx[j]
+                    right, right_scale = v_code[g][:, kp, :].bitcast(FP4X4), v_scale[g][:, kp, :]
                 else:
                     c = slice(P * i, P * (i + 1))
-                    lc, ls = e2_q[j][0][:, c], e2_q[j][1][:, c]
-                    rc, rs = w2_q[g][0][:].bitcast(FP8X4), w2_q[g][1][:]
+                    left = err2_mx[j]
+                    right, right_scale = w2_mx[g][0][:].bitcast(FP8X4), w2_mx[g][1][:]
                 nc.tensor.matmul_mx(
-                    out=acc[:], lhsT=lc.bitcast(FP8X4), lhsT_scale=ls, rhs=rc, rhs_scale=rs, start=(kp == 0), stop=(kp == 2)
+                    out=acc[:],
+                    lhsT=left[0][:, c].bitcast(FP8X4),
+                    lhsT_scale=left[1][:, c],
+                    rhs=right,
+                    rhs_scale=right_scale,
+                    start=(kp == 0),
+                    stop=(kp == 2),
                 )
 
-        masks_of, h_rows, h_words = {}, {}, {}
+        mask_of, h_rows, h_words, rounded_sums = {}, {}, {}, {}
 
-        def mask(s):
-            g, j = s // 8, s % 8
-            G, t0 = j // 2, 2 * (j % 2)
-            m = x_raw[(g, G)][:, t0 : t0 + 2, :]
-            masks_of[s] = m
+        def make_mask(n):
+            mask_of[n] = stage.tile([P, SLOTS, PASS], BF16, tag="mask", name="mask")
             nc.vector.tensor_tensor(
-                out=m,
-                in0=m,
-                in1=alpha_row[:, PASS * g : PASS * (g + 1)].unsqueeze(1).to_broadcast([P, 2, PASS]),
+                out=mask_of[n][:].rearrange("p t f -> p (t f)"),
+                in0=x_raw[(n // GROUPS, n % GROUPS)][:].rearrange("p t f -> p (t f)"),
+                in1=alpha_row[:, n // GROUPS, :, :].rearrange("p t f -> p (t f)"),
                 op=ALU.is_ge,
             )
 
-        def apply_mask(s, i):
-            hh, t = s // 2, 2 * (s % 2) + i
+        def empty_sums(s, i):
+            n, t = s // 2, 2 * (s % 2) + i
             if t == 0:
-                h_rows[hh] = stage.tile([P, 4, PASS], BF16, tag="h_rows", name="h_rows", bufs=2)
-            acc = bank_of[("s1", s, i)][1]
-            nc.vector.tensor_tensor(out=h_rows[hh][:, t, :], in0=acc[:], in1=masks_of[s][:, i, :], op=ALU.mult)
-            give_bank(("s1", s, i))
-
-        def interleave(hh, c0, c1, eng):
-            if c0 == 0:
-                h_words[hh] = stage.tile([P, 4 * PASS], BF16, tag="h_words", name="h_words", bufs=2, align_bytes=64)
-                h_q[hh] = planes("hq%d" % hh, PASS)
-            dst = h_words[hh][:, 4 * c0 : 4 * c1].rearrange("p (c i t) -> p c t i", i=4, t=4)
-            src = h_rows[hh][:, :, c0:c1].rearrange("p t (c i) -> p c t i", i=4)
-            if eng == "S":
-                nc.scalar.copy(out=dst, in_=src)
-            else:
-                nc.vector.tensor_copy(out=dst, in_=src)
-
-        def quant_h(hh, c0, c1):
-            quantise(h_q[hh][0][:, c0:c1], h_q[hh][1][:, c0:c1], h_words[hh][:, 4 * c0 : 4 * c1])
-
-        def mm2(g, rt, Gs):
-            if Gs[0] == 0:
-                take_bank(("s2", g, rt), [P, PASS])
-            acc = bank_of[("s2", g, rt)][1]
-            for G in Gs:
-                c = slice(P * G, P * (G + 1))
-                hq = h_q[4 * g + G]
-                nc.tensor.matmul_mx(
-                    out=acc[:], lhsT=sw_q[rt][0][:, c].bitcast(FP8X4), lhsT_scale=sw_q[rt][1][:, c],
-                    rhs=hq[0][:].bitcast(FP8X4), rhs_scale=hq[1][:], start=(G == 0), stop=(G == 3),
+                h_rows[n] = stage.tile([P, SLOTS, PASS], BF16, tag="h_rows", name="h_rows")
+            acc = held[("sums", s, i)][1]
+            if s not in SCALAR_EMPTIES:
+                nc.vector.tensor_tensor(out=h_rows[n][:, t, :], in0=acc[:], in1=mask_of[n][:, t, :], op=ALU.mult)
+                give_bank(("sums", s, i))
+                return
+            if i == 0:
+                rounded_sums[s] = stage.tile([P, 2, PASS], BF16, tag="sums", name="sums", bufs=1)
+            nc.scalar.copy(out=rounded_sums[s][:, i, :], in_=acc[:])
+            give_bank(("sums", s, i))
+            if i == 1:
+                both = slice(t - 1, t + 1)
+                nc.vector.tensor_tensor(
+                    out=h_rows[n][:, both, :], in0=rounded_sums[s][:], in1=mask_of[n][:, both, :], op=ALU.mult
                 )
 
-        y_f32, y_bf, y_turned, y_q = {}, {}, {}, {}
-
-        def finish_y(g, rt):
-            acc = bank_of[("s2", g, rt)][1]
-            y = stage.tile([P, PASS], F32, tag="y", name="y", bufs=4)
-            nc.vector.tensor_tensor(out=y[:], in0=acc[:], in1=bias_row[:, PASS * g : PASS * (g + 1)], op=ALU.add)
-            give_bank(("s2", g, rt))
-            nc.sync.dma_start(out=out_0[P * rt : P * (rt + 1), PASS * g : PASS * (g + 1)], in_=y[:])
-            y_f32[(g, rt)] = y
-
-        def round_y(g, rt):
-            y = y_f32[(g, rt)]
-            yb = stage.tile([P, 2, P, 2], BF16, tag="y_bf", name="y_bf", bufs=4)
-            y_bf[(g, rt)] = yb
-            nc.scalar.copy(out=yb[:], in_=y[:].rearrange("r (p u e) -> r u p e", u=2, e=2))
-
-        def round_y_from_psum(g, rt):
-            acc = bank_of[("s2", g, rt)][1]
-            yb = stage.tile([P, 2, P, 2], BF16, tag="y_bf", name="y_bf", bufs=4)
-            y_bf[(g, rt)] = yb
-            order = "r (p u e) -> r u p e"
-            nc.vector.tensor_tensor(
-                out=yb[:], in0=acc[:].rearrange(order, u=2, e=2),
-                in1=bias_row[:, PASS * g : PASS * (g + 1)].rearrange(order, u=2, e=2), op=ALU.add,
+        def interleave(n, c0, c1, copier):
+            if c0 == 0:
+                h_words[n] = stage.tile([P, SLOTS * PASS], BF16, tag="h_words", name="h_words", align_bytes=64)
+                h_mx[n] = mx_tiles("hq%d" % n, PASS)
+            copier(
+                out=h_words[n][:, SLOTS * c0 : SLOTS * c1].rearrange("p (c i t) -> p c t i", i=4, t=SLOTS),
+                in_=h_rows[n][:, :, c0:c1].rearrange("p t (c i) -> p c t i", i=4),
             )
 
-        def turn_y(g, rts, eng):
-            n = len(rts)
-            if rts[0] == 0:
-                y_turned[g] = stage.tile([P, 2048], BF16, tag="y_turned", name="y_turned", bufs=1, align_bytes=64)
-                y_q[g] = planes("yq%d" % g, R)
-            bank = take_bank("t", [P, n, 2, P])
-            for i in range(n):
-                words = y_bf[(g, rts[i])][:].rearrange("r u p e -> r u (p e)").bitcast(F32)
-                for u in range(2):
-                    nc.tensor.transpose(bank[:, i, u, :], words[:, u, :], ident[:])
-            dst = y_turned[g][:, PASS * rts[0] : PASS * (rts[-1] + 1)].bitcast(F32).rearrange("p (i r u) -> p i r u", i=n, u=2)
-            src = bank[:].rearrange("p i u r -> p i r u")
-            if eng == "S":
-                nc.scalar.copy(out=dst, in_=src)
-            else:
-                nc.vector.tensor_copy(out=dst, in_=src)
-            give_bank("t")
+        def quantise_h(n, c0, c1):
+            quantise(h_mx[n], slice(c0, c1), h_words[n][:, SLOTS * c0 : SLOTS * c1])
 
-        def quant_y(g, rts):
-            c = slice(P * rts[0], P * (rts[-1] + 1))
-            quantise(y_q[g][0][:, c], y_q[g][1][:, c], y_turned[g][:, PASS * rts[0] : PASS * (rts[-1] + 1)])
+        def half_tile(m):
+            return m // 2, HALF * (m % 2), HALF * (m % 2 + 1)
 
-        def store_words(g, rts):
-            c = slice(P * rts[0], P * (rts[-1] + 1))
-            dst = out_1[g].rearrange("p m t -> p (m t)").bitcast(I32)
-            nc.sync.dma_start(out=dst[:, c], in_=y_q[g][0][:, c].bitcast(I32))
-
-        def store_scales(g):
-            for Q in range(4):
-                eng = nc.sync if (g == 0 or Q % 2 == 0) else nc.scalar
-                eng.dma_start(
-                    out=out_2[g][4 * Q : 4 * Q + 4, :].bitcast(I32), in_=y_q[g][1][32 * Q : 32 * Q + 4, :].bitcast(I32)
+        def stage2(g, rt, groups):
+            if groups[0] == 0:
+                take_bank(("y", g, rt), [P, PASS])
+            acc = held[("y", g, rt)][1]
+            for G in groups:
+                c = slice(P * G, P * (G + 1))
+                h_tile = h_mx[GROUPS * g + G]
+                nc.tensor.matmul_mx(
+                    out=acc[:],
+                    lhsT=sw_mx[rt][0][:, c].bitcast(FP8X4),
+                    lhsT_scale=sw_mx[rt][1][:, c],
+                    rhs=h_tile[0][:].bitcast(FP8X4),
+                    rhs_scale=h_tile[1][:],
+                    start=(G == 0),
+                    stop=(G == GROUPS - 1),
                 )
 
-        e1_q[0] = planes("e1q0", 512)
-        first_bf = [stage.tile([P, PASS], BF16, tag="first_bf", name="first_bf", bufs=4, align_bytes=64) for n in range(4)]
+        y_f32, y_sorted, y_turned = {}, {}, {}
+        SORTED_ORDER = "r (p u e) -> r u p e"
 
-        def first_piece(src, i, kp):
-            turn("t", [src], first_bf[2 * i + kp][:])
-            c = slice(256 * i + P * kp, 256 * i + P * (kp + 1))
-            quantise(e1_q[0][0][:, c], e1_q[0][1][:, c], first_bf[2 * i + kp][:])
+        def small_tile(shape):
+            return stage.tile(shape, BF16, tag="small", name="small", bufs=4, align_bytes=64)
 
+        def store_y(g, rt):
+            y_f32[(g, rt)] = stage.tile([P, PASS], F32, tag="y", name="y", bufs=4)
+            y = y_f32[(g, rt)]
+            bias = bias_row[:, PASS * g : PASS * (g + 1)]
+            nc.vector.tensor_tensor(out=y[:], in0=held[("y", g, rt)][1][:], in1=bias, op=ALU.add)
+            give_bank(("y", g, rt))
+            nc.sync.dma_start(out=out_0[P * rt : P * (rt + 1), PASS * g : PASS * (g + 1)], in_=y[:])
+
+        def round_y(g, rt):
+            y_sorted[(g, rt)] = small_tile([P, 2, P, 2])
+            nc.scalar.copy(out=y_sorted[(g, rt)][:], in_=y_f32[(g, rt)][:].rearrange(SORTED_ORDER, u=2, e=2))
+
+        def round_y_from_psum(g, rt):
+            y_sorted[(g, rt)] = small_tile([P, 2, P, 2])
+            nc.vector.tensor_tensor(
+                out=y_sorted[(g, rt)][:],
+                in0=held[("y", g, rt)][1][:].rearrange(SORTED_ORDER, u=2, e=2),
+                in1=bias_row[:, PASS * g : PASS * (g + 1)].rearrange(SORTED_ORDER, u=2, e=2),
+                op=ALU.add,
+            )
+
+        def turn_y(g, rt0, n, copier):
+            if rt0 == 0:
+                y_turned[g] = stage.tile([P, SLOTS * R], BF16, tag="y_turned", name="y_turned", bufs=1, align_bytes=64)
+                y_mx[g] = mx_tiles("yq%d" % g, R)
+            bank = take_bank("turn", [P, n, 2, P])
+            for i in range(n):
+                pairs = y_sorted[(g, rt0 + i)][:].rearrange("r u p e -> r u (p e)").bitcast(F32)
+                for u in range(2):
+                    nc.tensor.transpose(bank[:, i, u, :], pairs[:, u, :], ident[:])
+            dst = y_turned[g][:, PASS * rt0 : PASS * (rt0 + n)].bitcast(F32)
+            copier(out=dst.rearrange("p (i r u) -> p i r u", i=n, u=2), in_=bank[:].rearrange("p i u r -> p i r u"))
+            give_bank("turn")
+
+        def quantise_y(g, rt0, n):
+            quantise(y_mx[g], slice(P * rt0, P * (rt0 + n)), y_turned[g][:, PASS * rt0 : PASS * (rt0 + n)])
+
+        def store_codes(g, rt0, n):
+            c = slice(P * rt0, P * (rt0 + n))
+            dst = out_1[g].rearrange("p m t -> p (m t)").bitcast(I32)
+            nc.sync.dma_start(out=dst[:, c], in_=y_mx[g][0][:, c].bitcast(I32))
+
+        def store_scales(g, queues):
+            for Q in range(4):
+                queues[Q % len(queues)].dma_start(
+                    out=out_2[g][4 * Q : 4 * Q + 4, :].bitcast(I32),
+                    in_=y_mx[g][1][32 * Q : 32 * Q + 4, :].bitcast(I32),
+                )
+
+        err1_mx[0] = mx_tiles("e1q0", PASS)
+        first_turned = [small_tile([P, PASS]) for piece in range(4)]
         spread_alpha()
-        copy_alpha()
         for i in range(2):
             for kp in range(2):
-                first_piece(e1_raw[(0, i)][:, PASS * kp : PASS * (kp + 1)], i, kp)
-        mm1(0, 0, [0, 1])
-        mm1(0, 1, [0, 1])
-        sort_e1(1, 0, "S")
-        sort_e1(1, 1, "S")
-        sort_w2(0, 0, "V")
-        sort_w2(0, 1, "V")
-        sort_e2(0, "V")
-        turn_e1(1, 0)
-        turn_e1(1, 1)
-        sort_e2(1, "V")
-        quant_e1_half(1, 0)
-        quant_e1_half(1, 1)
-        turn_w2(0, 0)
-        turn_w2(0, 1)
-        turn_e2(0)
-        turn_e2(1)
-        mm1(1, 0, [0, 1])
-        mm1(1, 1, [0, 1])
-        sort_e2(2, "V")
-        quant_w2(0)
-        quant_e2(0)
-        mask(0)
-        quant_e2(1)
-        load_x(1, 0)
-        turn_e1(2, 0)
-        turn_e1(2, 1)
-        turn_e2(2)
-        mask(1)
+                piece = first_turned[2 * i + kp]
+                turn(("first", i, kp), [err1_slot(0, i)[:, PASS * kp : PASS * (kp + 1)]], piece[:])
+                quantise(err1_mx[0], slice(HALF * i + P * kp, HALF * i + P * (kp + 1)), piece[:])
+        for i in range(2):
+            stage1(0, i, [0, 1])
+        repeat_alpha()
+        for i in range(2):
+            sort_pairs(("err1", 1, i), err1_slot(1, i), scalar_copy)
+        for h in range(2):
+            sort_pairs(("w2", 0, h), w2_raw[0][:, 2 * h : 2 * h + 2, :].rearrange("p j k -> p (j k)"), vector_copy)
+        turn_err1(1)
+        for j in range(2):
+            sort_err2(j, vector_copy)
+        for i in range(2):
+            src = turned[("err1", 1)][:, 2 * PASS * i : 2 * PASS * (i + 1)]
+            quantise(err1_mx[1], slice(HALF * i, HALF * (i + 1)), src)
+        turn_w2(0)
+        for j in range(2):
+            turn_err2(j)
+        for i in range(2):
+            stage1(1, i, [0, 1])
+        quantise_w2(0)
+        quantise_err2(0)
+        make_mask(0)
+        quantise_err2(1)
+        turn_err1(2)
+        turn_err2(2)
         for s in range(2):
             for i in range(2):
-                mm1(s, i, [2])
-        apply_mask(0, 0)
-        quant_e1(2)
-        apply_mask(0, 1)
-        quant_e2(2)
-        apply_mask(1, 0)
+                stage1(s, i, [2])
+        empty_sums(0, 0)
+        quantise_err1(2)
+        empty_sums(0, 1)
+        quantise_err2(2)
+        empty_sums(1, 0)
 
-        sorter = {"e2": sort_e2, "w2": sort_w2, "sw": sort_sw, "e1": sort_e1}
-        next_mask = [2]
-
-        def masks_to(n):
-            while next_mask[0] <= min(n, 15):
-                mask(next_mask[0])
-                next_mask[0] = next_mask[0] + 1
-
-        def half(n):
-            return n // 2, 256 * (n % 2), 256 * (n % 2 + 1)
-
-        for s in range(2, 11):
-            if s > 0:
-                apply_mask(s - 1, 1)
-                masks_to(MASK_AHEAD[s])
+        for s in range(2, STAGE2_STEP):
+            empty_sums(s - 1, 1)
+            if s % 2 == 0:
+                make_mask(s // 2)
             if s >= 3:
-                quant_h(*half(s - 3))
-            if s < 7:
-                turn_e1(s + 1, 0)
-                turn_e1(s + 1, 1)
-                turn_e2(s + 1)
-                if s % 2 == 0:
+                quantise_h(*half_tile(s - 3))
+            if s <= LAST_ERR_STEP:
+                turn_err1(s + 1)
+                turn_err2(s + 1)
+                if s == 3:
+                    load_sw(0)
+                    load_x(1, 0)
+                    load_sw(1)
+                    load_sw(2)
+                    load_x(1, 1)
+                    load_sw(3)
+                if s > 3 and s % 2 == 0:
                     load_x(1, s // 2)
-                quant_e1(s + 1)
-                quant_e2(s + 1)
-            elif s == 7:
-                turn_w2(1, 0)
-                turn_w2(1, 1)
-                quant_w2(1)
-                nc.vector.tensor_tensor(out=bias_col[:], in0=reg_col[:], in1=al_col[:], op=ALU.mult)
-                turn_sw(0)
-                quant_sw(0)
+                quantise_err1(s + 1)
+                quantise_err2(s + 1)
             else:
-                turn_sw(s - 7)
-                if s < 10:
-                    spread_bias(s - 8)
-                quant_sw(s - 7)
-            for item in SORTS.get(s, []):
-                sorter[item[0]](*item[1:])
-            if s >= 2:
-                interleave(*half(s - 2), "S")
-            mm1(s, 0, [0, 1, 2])
-            mm1(s, 1, [0, 1, 2])
-            apply_mask(s, 0)
+                rt = s - W2_STEP
+                if rt == 0:
+                    turn_w2(1)
+                    quantise_w2(1)
+                    nc.vector.tensor_tensor(out=bias_col[:], in0=reg_col[:], in1=alpha_col[:], op=ALU.mult)
+                turn_sw(rt)
+                if rt in (1, 2):
+                    spread_bias(rt - 1)
+                quantise_sw(rt)
+            if s + 2 in SCALAR_SORTS:
+                sort_err2(s + 2, scalar_copy)
+            interleave(*half_tile(s - 2), scalar_copy)
+            for i in range(2):
+                stage1(s, i, [0, 1, 2])
+            empty_sums(s, 0)
 
-        for s in range(11, 16):
-            apply_mask(s - 1, 1)
-            if s == 11:
-                interleave(*half(s - 2), "S")
+        for s in range(STAGE2_STEP, LAST_STEP + 1):
+            rt = s - STAGE2_STEP
+            done = s // 2 - 1
+            empty_sums(s - 1, 1)
+            if rt == 0:
+                interleave(done, HALF, PASS, scalar_copy)
             elif s % 2 == 0:
-                interleave((s - 2) // 2, 0, 256, "S")
-            if s >= 12:
-                finish_y(0, s - 12)
-                round_y(0, s - 12)
-            masks_to(MASK_AHEAD[s])
-            if s >= 12 and s % 2 == 0:
-                interleave((s - 2) // 2, 256, 512, "S")
-            if s <= 12:
-                quant_h(*half(s - 3))
-            elif s == 13:
-                quant_h(5, 0, 512)
-            elif s == 15:
-                quant_h(6, 0, 256)
-            mm1(s, 0, [0, 1, 2])
-            mm1(s, 1, [0, 1, 2])
-            if s <= 14:
-                mm2(0, s - 11, [0, 1, 2, 3])
-            if s == 14:
-                turn_y(0, [0, 1], "S")
-            apply_mask(s, 0)
+                interleave(done, 0, HALF, scalar_copy)
+            if rt > 0:
+                store_y(0, rt - 1)
+                round_y(0, rt - 1)
+            if s % 2 == 1 and s < LAST_STEP:
+                make_mask((s + 1) // 2)
+            if s % 2 == 0:
+                interleave(done, HALF, PASS, scalar_copy)
+            if rt <= 1:
+                quantise_h(*half_tile(s - 3))
+            elif s == LAST_STEP:
+                quantise_h(done, 0, HALF)
+            elif s % 2 == 1:
+                quantise_h(done, 0, PASS)
+            for i in range(2):
+                stage1(s, i, [0, 1, 2])
+            if rt < ROW_TILES:
+                stage2(0, rt, range(GROUPS))
+            if rt == ROW_TILES - 1:
+                turn_y(0, 0, 2, scalar_copy)
+            empty_sums(s, 0)
 
+        last = 2 * GROUPS - 1
         for rt in range(3):
-            mm2(1, rt, [0, 1])
-        quant_h(6, 256, 512)
-        apply_mask(15, 1)
-        interleave(7, 0, 160, "S")
-        interleave(7, 160, 512, "V")
-        turn_y(0, [2, 3], "S")
+            stage2(1, rt, [0, 1])
+        quantise_h(last - 1, HALF, PASS)
+        empty_sums(LAST_STEP, 1)
+        interleave(last, 0, TAIL_SCALAR_COLUMNS, scalar_copy)
+        interleave(last, TAIL_SCALAR_COLUMNS, PASS, vector_copy)
+        turn_y(0, 2, 2, scalar_copy)
         for rt in range(2):
-            mm2(1, rt, [2])
-        quant_h(7, 0, 512)
+            stage2(1, rt, [2])
+        quantise_h(last, 0, PASS)
         for rt in range(2):
-            mm2(1, rt, [3])
-        mm2(1, 2, [2, 3])
-        mm2(1, 3, [0, 1, 2, 3])
-        quant_y(0, [0, 1])
-        quant_y(0, [2, 3])
-        store_words(0, [0, 1, 2, 3])
-        store_scales(0)
+            stage2(1, rt, [3])
+        stage2(1, 2, [2, 3])
+        stage2(1, 3, range(GROUPS))
+        quantise_y(0, 0, 2)
+        quantise_y(0, 2, 2)
+        store_codes(0, 0, ROW_TILES)
+        store_scales(0, [nc.sync])
         for rt in range(3):
-            finish_y(1, rt)
+            store_y(1, rt)
             round_y(1, rt)
         round_y_from_psum(1, 3)
-        finish_y(1, 3)
-        turn_y(1, [0, 1], "S")
-        turn_y(1, [3], "V")
-        turn_y(1, [2], "S")
-        quant_y(1, [0, 1])
-        store_words(1, [0, 1])
-        quant_y(1, [2, 3])
-        store_words(1, [2, 3])
-        store_scales(1)
+        store_y(1, 3)
+        turn_y(1, 0, 2, scalar_copy)
+        turn_y(1, 3, 1, vector_copy)
+        turn_y(1, 2, 1, scalar_copy)
+        quantise_y(1, 0, 2)
+        store_codes(1, 0, 2)
+        quantise_y(1, 2, 2)
+        store_codes(1, 2, 2)
+        store_scales(1, [nc.sync, nc.scalar])

from contextlib import ExitStack

import concourse.mybir as mybir
from concourse.masks import make_identity

T, K1, K2, F, R = 2048, 1024, 512, 1024, 512
FLOPS = 2 * T * (K1 + K2) * F + 2 * R * T * F

F32 = mybir.dt.float32
BF16 = mybir.dt.bfloat16
U8 = mybir.dt.uint8
U32 = mybir.dt.uint32
I32 = mybir.dt.int32
FP8X4 = mybir.dt.float8_e4m3fn_x4
FP4X4 = mybir.dt.float4_e2m1fn_x4
ALU = mybir.AluOpType

P = 128
PASS = 512
HALF = PASS // 2
SLOTS = 4
GROUPS = T // PASS
PAIRS = 2 * GROUPS
ROW_TILES = R // P
BANKS = 8

LAST_ERR_STEP = PAIRS - 2
W2_STEP = PAIRS - 1
STAGE2_STEP = W2_STEP + ROW_TILES
LAST_STEP = 2 * PAIRS - 1
SCALAR_EMPTIES = (1, STAGE2_STEP, STAGE2_STEP + 2)
SCALAR_SORTS = (4, 6)
TAIL_SCALAR_COLUMNS = 160


def tile_pact_threshold_gradient_k6_kernel(
    tc, err1, v_words, v_scales, err2, w2, x, alpha, sample_w, reg, out_0, out_1, out_2
):
    nc = tc.nc
    with ExitStack() as ctx:
        keep = ctx.enter_context(tc.tile_pool(name="keep", bufs=1))
        stage = ctx.enter_context(tc.tile_pool(name="stage", bufs=2))
        psum = ctx.enter_context(tc.psum_pool(name="psum", bufs=1))
        ctx.enter_context(tc.manual_schedule())

        free_banks = list(range(BANKS))
        held = {}

        def take_bank(key, shape):
            b = free_banks.pop(0)
            bank = psum.tile(shape, F32, tag="bank%d" % b, name="bank%d" % b)
            held[key] = (b, bank)
            return bank

        def give_bank(key):
            free_banks.append(held.pop(key)[0])

        def kept(name, shape, dtype):
            return keep.tile(shape, dtype, name=name, tag=name, align_bytes=64)

        def mx_tiles(name, columns):
            return kept(name + "_c", [P, columns], U32), kept(name + "_s", [P, columns], U8)

        scalar_copy, vector_copy = nc.scalar.copy, nc.vector.tensor_copy

        def quantise(tiles, columns, src):
            nc.vector.quantize_mx(out=tiles[0][:, columns].bitcast(FP8X4), scales=tiles[1][:, columns], in_=src)

        ident = kept("ident", [P, P], F32)
        make_identity(nc, ident[:])
        v_scale = [kept("v_sc%d" % g, [P, 2, PASS], U8) for g in range(2)]
        for g in range(2):
            nc.vector.memset(v_scale[g][:].rearrange("p k n -> p (k n)").bitcast(I32), 0)

        err1_raw, err2_raw, x_raw, sw_raw, w2_raw, v_code = {}, {}, {}, {}, {}, {}
        err1_v = err1.rearrange("(G p t) k -> G p t k", p=P, t=SLOTS)
        err2_v = err2.rearrange("(G p t) k -> G p t k", p=P, t=SLOTS)
        x_v = x.rearrange("(G p t) f -> G p t f", p=P, t=SLOTS)

        def load_err1(G, t0, n):
            tl = kept("e1r_%d_%d" % (G, t0), [P, n, K1], BF16)
            nc.sync.dma_start(out=tl[:], in_=err1_v[G][:, t0 : t0 + n, :])
            for i in range(n):
                err1_raw[(G, t0 + i)] = tl[:, i, :]

        def load_err2(j):
            t0 = 2 * (j % 2)
            err2_raw[j] = kept("e2r_%d" % j, [P, 2, K2], BF16)
            nc.sync.dma_start(out=err2_raw[j][:], in_=err2_v[j // 2][:, t0 : t0 + 2, :])

        def load_x(g, G):
            x_raw[(g, G)] = kept("xr_%d" % G if g == 0 else "e1r_%d_2" % G, [P, SLOTS, PASS], BF16)
            nc.sync.dma_start(out=x_raw[(g, G)][:], in_=x_v[G][:, :, PASS * g : PASS * (g + 1)])

        def load_w2(g):
            w2_raw[g] = kept("w2r_%d" % g, [P, 4, K2], BF16)
            nc.sync.dma_start(
                out=w2_raw[g][:], in_=w2[PASS * g : PASS * (g + 1), :].rearrange("(p j) k -> p j k", p=P)
            )

        def load_sw(rt):
            sw_raw[rt] = kept("e1r_%d_0" % (rt + 1) if rt < 2 else "swr_%d" % rt, [P, T], BF16)
            nc.sync.dma_start(out=sw_raw[rt][:], in_=sample_w[P * rt : P * (rt + 1), :])

        def load_v(g):
            v_code[g] = kept("vw_%d" % g, [P, 2, 2 * PASS], U8)
            src = v_words.rearrange("k p n -> p k n")[:, :, 2 * PASS * g : 2 * PASS * (g + 1)]
            nc.sync.dma_start(out=v_code[g][:].bitcast(I32), in_=src.bitcast(I32))

        def load_v_scales(g):
            src = v_scales.rearrange("k q n -> q k n")[:, :, PASS * g : PASS * (g + 1)]
            for Q in range(4):
                nc.sync.dma_start(
                    out=v_scale[g][32 * Q : 32 * Q + 4, :, :].bitcast(I32),
                    in_=src[4 * Q : 4 * Q + 4, :, :].bitcast(I32),
                )

        alpha_col = kept("al_col", [P, 8], BF16)
        reg_col = kept("reg_col", [P, 8], BF16)

        nc.sync.dma_start(out=alpha_col[:], in_=alpha.rearrange("(p c) -> p c", c=8))
        load_err1(0, 0, 1)
        load_err1(0, 1, 1)
        load_v_scales(0)
        load_v(0)
        load_err1(0, 2, 2)
        load_w2(0)
        load_err2(0)
        load_err2(1)
        for G in range(1, GROUPS):
            load_err1(G, 0, 2)
            if G == 1:
                load_x(0, 0)
            load_err2(2 * G)
            load_err1(G, 2, 2)
            load_err2(2 * G + 1)
            load_x(0, G)
        load_w2(1)
        load_v(1)
        load_v_scales(1)
        nc.sync.dma_start(out=reg_col[:], in_=reg.rearrange("(p c) -> p c", c=8))

        err1_mx, err2_mx, w2_mx, sw_mx, h_mx, y_mx = {}, {}, {}, {}, {}, {}
        turned, sorted_pairs = {}, {}

        def sort_pairs(key, src, copier):
            dst = stage.tile([P, 2 * PASS], BF16, tag="sorted", name="sorted", bufs=4)
            copier(
                out=dst[:].bitcast(F32).rearrange("r (i u p) -> r i u p", i=2, u=2),
                in_=src.bitcast(F32).rearrange("r (i p u) -> r i u p", i=2, u=2),
            )
            sorted_pairs[key] = dst

        def transpose_runs(key, runs):
            is_sorted = key in sorted_pairs
            if is_sorted:
                runs = [sorted_pairs[key][:, PASS * i : PASS * (i + 1)] for i in range(2)]
            bank = take_bank("turn", [P, len(runs), 2, P])
            for i, run in enumerate(runs):
                pairs = run.bitcast(F32)
                for u in range(2):
                    part = pairs[:, P * u : P * (u + 1)] if is_sorted else pairs[:, u : 2 * P : 2]
                    nc.tensor.transpose(bank[:, i, u, :], part, ident[:])
            return bank

        def turn(key, runs, dst):
            bank = transpose_runs(key, runs)
            nc.scalar.copy(
                out=dst.bitcast(F32).rearrange("p (i r u) -> p i r u", i=len(runs), u=2),
                in_=bank[:].rearrange("p i u r -> p i r u"),
            )
            give_bank("turn")

        def wide_tile():
            return stage.tile([P, 4 * PASS], BF16, tag="wide", name="wide", align_bytes=64)

        def err1_slot(j, i):
            return err1_raw[(j // 2, 2 * (j % 2) + i)]

        def turn_err1(j):
            turned[("err1", j)] = wide_tile()
            err1_mx[j] = mx_tiles("e1q%d" % j, PASS)
            for i in range(2):
                raw = err1_slot(j, i)
                dst = turned[("err1", j)][:, 2 * PASS * i : 2 * PASS * (i + 1)]
                turn(("err1", j, i), [raw[:, 0:PASS], raw[:, PASS : 2 * PASS]], dst)

        def quantise_err1(j):
            quantise(err1_mx[j], slice(0, PASS), turned[("err1", j)][:])

        def turn_err2(j):
            turned[("err2", j)] = stage.tile([P, 2 * PASS], BF16, tag="e2b", name="e2b", align_bytes=64)
            err2_mx[j] = mx_tiles("e2q%d" % j, HALF)
            turn(("err2", j), [err2_raw[j][:, 0, :], err2_raw[j][:, 1, :]], turned[("err2", j)][:])

        def sort_err2(j, copier):
            sort_pairs(("err2", j), err2_raw[j][:].rearrange("p t k -> p (t k)"), copier)

        def quantise_err2(j):
            quantise(err2_mx[j], slice(0, HALF), turned[("err2", j)][:])

        def turn_w2(g):
            turned[("w2", g)] = wide_tile()
            w2_mx[g] = mx_tiles("w2q%d" % g, PASS)
            by_channel = turned[("w2", g)][:].bitcast(F32).rearrange("p (r j u) -> p r j u", j=4, u=2)
            for h in range(2):
                bank = transpose_runs(("w2", g, h), [w2_raw[g][:, 2 * h, :], w2_raw[g][:, 2 * h + 1, :]])
                nc.scalar.copy(out=by_channel[:, :, 2 * h : 2 * h + 2, :], in_=bank[:].rearrange("p j u r -> p r j u"))
                give_bank("turn")

        def quantise_w2(g):
            quantise(w2_mx[g], slice(0, PASS), turned[("w2", g)][:])

        def turn_sw(rt):
            turned[("sw", rt)] = wide_tile()
            sw_mx[rt] = mx_tiles("swq%d" % rt, PASS)
            for h in range(2):
                runs = [sw_raw[rt][:, PASS * G : PASS * (G + 1)] for G in (2 * h, 2 * h + 1)]
                turn(("sw", rt, h), runs, turned[("sw", rt)][:, 2 * PASS * h : 2 * PASS * (h + 1)])

        def quantise_sw(rt):
            quantise(sw_mx[rt], slice(0, PASS), turned[("sw", rt)][:])

        alpha_row = kept("alpha_row", [P, 2, SLOTS, PASS], BF16)
        bias_row = kept("bias_row", [P, F], F32)
        bias_col = kept("bias_col", [P, 8], F32)

        def spread_alpha():
            bank = take_bank("turn", [P, 4, P])
            pairs = alpha_col[:].bitcast(F32)
            for w in range(4):
                nc.tensor.transpose(bank[:, w, :], pairs[:, w : w + 1].to_broadcast([P, P]), ident[:])
            nc.vector.tensor_copy(
                out=alpha_row[:, :, 0, :].bitcast(F32).rearrange("p g (n w) -> p g n w", w=4),
                in_=bank[:].rearrange("p w (g n) -> p g n w", g=2),
            )
            give_bank("turn")

        def repeat_alpha():
            nc.vector.tensor_copy(
                out=alpha_row[:, :, 1:SLOTS, :], in_=alpha_row[:, :, 0:1, :].to_broadcast([P, 2, SLOTS - 1, PASS])
            )

        def spread_bias(h):
            bank = take_bank("turn", [P, 4, P])
            for c in range(4):
                column = bias_col[:, 4 * h + c : 4 * h + c + 1]
                nc.tensor.transpose(bank[:, c, :], column.to_broadcast([P, P]), ident[:])
            nc.scalar.copy(
                out=bias_row[:].rearrange("p (n c) -> p n c", c=8)[:, :, 4 * h : 4 * h + 4],
                in_=bank[:].rearrange("p c n -> p n c"),
            )
            give_bank("turn")

        def stage1(s, i, passes):
            g, j = s // PAIRS, s % PAIRS
            if passes[0] == 0:
                take_bank(("sums", s, i), [P, PASS])
            acc = held[("sums", s, i)][1]
            for kp in passes:
                if kp < 2:
                    c = slice(HALF * i + P * kp, HALF * i + P * (kp + 1))
                    left = err1_mx[j]
                    right, right_scale = v_code[g][:, kp, :].bitcast(FP4X4), v_scale[g][:, kp, :]
                else:
                    c = slice(P * i, P * (i + 1))
                    left = err2_mx[j]
                    right, right_scale = w2_mx[g][0][:].bitcast(FP8X4), w2_mx[g][1][:]
                nc.tensor.matmul_mx(
                    out=acc[:],
                    lhsT=left[0][:, c].bitcast(FP8X4),
                    lhsT_scale=left[1][:, c],
                    rhs=right,
                    rhs_scale=right_scale,
                    start=(kp == 0),
                    stop=(kp == 2),
                )

        mask_of, h_rows, h_words, rounded_sums = {}, {}, {}, {}

        def make_mask(n):
            mask_of[n] = stage.tile([P, SLOTS, PASS], BF16, tag="mask", name="mask")
            nc.vector.tensor_tensor(
                out=mask_of[n][:].rearrange("p t f -> p (t f)"),
                in0=x_raw[(n // GROUPS, n % GROUPS)][:].rearrange("p t f -> p (t f)"),
                in1=alpha_row[:, n // GROUPS, :, :].rearrange("p t f -> p (t f)"),
                op=ALU.is_ge,
            )

        def empty_sums(s, i):
            n, t = s // 2, 2 * (s % 2) + i
            if t == 0:
                h_rows[n] = stage.tile([P, SLOTS, PASS], BF16, tag="h_rows", name="h_rows")
            acc = held[("sums", s, i)][1]
            if s not in SCALAR_EMPTIES:
                nc.vector.tensor_tensor(out=h_rows[n][:, t, :], in0=acc[:], in1=mask_of[n][:, t, :], op=ALU.mult)
                give_bank(("sums", s, i))
                return
            if i == 0:
                rounded_sums[s] = stage.tile([P, 2, PASS], BF16, tag="sums", name="sums", bufs=1)
            nc.scalar.copy(out=rounded_sums[s][:, i, :], in_=acc[:])
            give_bank(("sums", s, i))
            if i == 1:
                both = slice(t - 1, t + 1)
                nc.vector.tensor_tensor(
                    out=h_rows[n][:, both, :], in0=rounded_sums[s][:], in1=mask_of[n][:, both, :], op=ALU.mult
                )

        def interleave(n, c0, c1, copier):
            if c0 == 0:
                h_words[n] = stage.tile([P, SLOTS * PASS], BF16, tag="h_words", name="h_words", align_bytes=64)
                h_mx[n] = mx_tiles("hq%d" % n, PASS)
            copier(
                out=h_words[n][:, SLOTS * c0 : SLOTS * c1].rearrange("p (c i t) -> p c t i", i=4, t=SLOTS),
                in_=h_rows[n][:, :, c0:c1].rearrange("p t (c i) -> p c t i", i=4),
            )

        def quantise_h(n, c0, c1):
            quantise(h_mx[n], slice(c0, c1), h_words[n][:, SLOTS * c0 : SLOTS * c1])

        def half_tile(m):
            return m // 2, HALF * (m % 2), HALF * (m % 2 + 1)

        def stage2(g, rt, groups):
            if groups[0] == 0:
                take_bank(("y", g, rt), [P, PASS])
            acc = held[("y", g, rt)][1]
            for G in groups:
                c = slice(P * G, P * (G + 1))
                h_tile = h_mx[GROUPS * g + G]
                nc.tensor.matmul_mx(
                    out=acc[:],
                    lhsT=sw_mx[rt][0][:, c].bitcast(FP8X4),
                    lhsT_scale=sw_mx[rt][1][:, c],
                    rhs=h_tile[0][:].bitcast(FP8X4),
                    rhs_scale=h_tile[1][:],
                    start=(G == 0),
                    stop=(G == GROUPS - 1),
                )

        y_f32, y_sorted, y_turned = {}, {}, {}
        SORTED_ORDER = "r (p u e) -> r u p e"

        def small_tile(shape):
            return stage.tile(shape, BF16, tag="small", name="small", bufs=4, align_bytes=64)

        def store_y(g, rt):
            y_f32[(g, rt)] = stage.tile([P, PASS], F32, tag="y", name="y", bufs=4)
            y = y_f32[(g, rt)]
            bias = bias_row[:, PASS * g : PASS * (g + 1)]
            nc.vector.tensor_tensor(out=y[:], in0=held[("y", g, rt)][1][:], in1=bias, op=ALU.add)
            give_bank(("y", g, rt))
            nc.sync.dma_start(out=out_0[P * rt : P * (rt + 1), PASS * g : PASS * (g + 1)], in_=y[:])

        def round_y(g, rt):
            y_sorted[(g, rt)] = small_tile([P, 2, P, 2])
            nc.scalar.copy(out=y_sorted[(g, rt)][:], in_=y_f32[(g, rt)][:].rearrange(SORTED_ORDER, u=2, e=2))

        def round_y_from_psum(g, rt):
            y_sorted[(g, rt)] = small_tile([P, 2, P, 2])
            nc.vector.tensor_tensor(
                out=y_sorted[(g, rt)][:],
                in0=held[("y", g, rt)][1][:].rearrange(SORTED_ORDER, u=2, e=2),
                in1=bias_row[:, PASS * g : PASS * (g + 1)].rearrange(SORTED_ORDER, u=2, e=2),
                op=ALU.add,
            )

        def turn_y(g, rt0, n, copier):
            if rt0 == 0:
                y_turned[g] = stage.tile([P, SLOTS * R], BF16, tag="y_turned", name="y_turned", bufs=1, align_bytes=64)
                y_mx[g] = mx_tiles("yq%d" % g, R)
            bank = take_bank("turn", [P, n, 2, P])
            for i in range(n):
                pairs = y_sorted[(g, rt0 + i)][:].rearrange("r u p e -> r u (p e)").bitcast(F32)
                for u in range(2):
                    nc.tensor.transpose(bank[:, i, u, :], pairs[:, u, :], ident[:])
            dst = y_turned[g][:, PASS * rt0 : PASS * (rt0 + n)].bitcast(F32)
            copier(out=dst.rearrange("p (i r u) -> p i r u", i=n, u=2), in_=bank[:].rearrange("p i u r -> p i r u"))
            give_bank("turn")

        def quantise_y(g, rt0, n):
            quantise(y_mx[g], slice(P * rt0, P * (rt0 + n)), y_turned[g][:, PASS * rt0 : PASS * (rt0 + n)])

        def store_codes(g, rt0, n):
            c = slice(P * rt0, P * (rt0 + n))
            dst = out_1[g].rearrange("p m t -> p (m t)").bitcast(I32)
            nc.sync.dma_start(out=dst[:, c], in_=y_mx[g][0][:, c].bitcast(I32))

        def store_scales(g, queues):
            for Q in range(4):
                queues[Q % len(queues)].dma_start(
                    out=out_2[g][4 * Q : 4 * Q + 4, :].bitcast(I32),
                    in_=y_mx[g][1][32 * Q : 32 * Q + 4, :].bitcast(I32),
                )

        err1_mx[0] = mx_tiles("e1q0", PASS)
        first_turned = [small_tile([P, PASS]) for piece in range(4)]
        spread_alpha()
        for i in range(2):
            for kp in range(2):
                piece = first_turned[2 * i + kp]
                turn(("first", i, kp), [err1_slot(0, i)[:, PASS * kp : PASS * (kp + 1)]], piece[:])
                quantise(err1_mx[0], slice(HALF * i + P * kp, HALF * i + P * (kp + 1)), piece[:])
        for i in range(2):
            stage1(0, i, [0, 1])
        repeat_alpha()
        for i in range(2):
            sort_pairs(("err1", 1, i), err1_slot(1, i), scalar_copy)
        for h in range(2):
            sort_pairs(("w2", 0, h), w2_raw[0][:, 2 * h : 2 * h + 2, :].rearrange("p j k -> p (j k)"), vector_copy)
        turn_err1(1)
        for j in range(2):
            sort_err2(j, vector_copy)
        for i in range(2):
            src = turned[("err1", 1)][:, 2 * PASS * i : 2 * PASS * (i + 1)]
            quantise(err1_mx[1], slice(HALF * i, HALF * (i + 1)), src)
        turn_w2(0)
        for j in range(2):
            turn_err2(j)
        for i in range(2):
            stage1(1, i, [0, 1])
        quantise_w2(0)
        quantise_err2(0)
        make_mask(0)
        quantise_err2(1)
        turn_err1(2)
        turn_err2(2)
        for s in range(2):
            for i in range(2):
                stage1(s, i, [2])
        empty_sums(0, 0)
        quantise_err1(2)
        empty_sums(0, 1)
        quantise_err2(2)
        empty_sums(1, 0)

        for s in range(2, STAGE2_STEP):
            empty_sums(s - 1, 1)
            if s % 2 == 0:
                make_mask(s // 2)
            if s >= 3:
                quantise_h(*half_tile(s - 3))
            if s <= LAST_ERR_STEP:
                turn_err1(s + 1)
                turn_err2(s + 1)
                if s == 3:
                    load_sw(0)
                    load_x(1, 0)
                    load_sw(1)
                    load_sw(2)
                    load_x(1, 1)
                    load_sw(3)
                if s > 3 and s % 2 == 0:
                    load_x(1, s // 2)
                quantise_err1(s + 1)
                quantise_err2(s + 1)
            else:
                rt = s - W2_STEP
                if rt == 0:
                    turn_w2(1)
                    quantise_w2(1)
                    nc.vector.tensor_tensor(out=bias_col[:], in0=reg_col[:], in1=alpha_col[:], op=ALU.mult)
                turn_sw(rt)
                if rt in (1, 2):
                    spread_bias(rt - 1)
                quantise_sw(rt)
            if s + 2 in SCALAR_SORTS:
                sort_err2(s + 2, scalar_copy)
            interleave(*half_tile(s - 2), scalar_copy)
            for i in range(2):
                stage1(s, i, [0, 1, 2])
            empty_sums(s, 0)

        for s in range(STAGE2_STEP, LAST_STEP + 1):
            rt = s - STAGE2_STEP
            done = s // 2 - 1
            empty_sums(s - 1, 1)
            if rt == 0:
                interleave(done, HALF, PASS, scalar_copy)
            elif s % 2 == 0:
                interleave(done, 0, HALF, scalar_copy)
            if rt > 0:
                store_y(0, rt - 1)
                round_y(0, rt - 1)
            if s % 2 == 1 and s < LAST_STEP:
                make_mask((s + 1) // 2)
            if s % 2 == 0:
                interleave(done, HALF, PASS, scalar_copy)
            if rt <= 1:
                quantise_h(*half_tile(s - 3))
            elif s == LAST_STEP:
                quantise_h(done, 0, HALF)
            elif s % 2 == 1:
                quantise_h(done, 0, PASS)
            for i in range(2):
                stage1(s, i, [0, 1, 2])
            if rt < ROW_TILES:
                stage2(0, rt, range(GROUPS))
            if rt == ROW_TILES - 1:
                turn_y(0, 0, 2, scalar_copy)
            empty_sums(s, 0)

        last = 2 * GROUPS - 1
        for rt in range(3):
            stage2(1, rt, [0, 1])
        quantise_h(last - 1, HALF, PASS)
        empty_sums(LAST_STEP, 1)
        interleave(last, 0, TAIL_SCALAR_COLUMNS, scalar_copy)
        interleave(last, TAIL_SCALAR_COLUMNS, PASS, vector_copy)
        turn_y(0, 2, 2, scalar_copy)
        for rt in range(2):
            stage2(1, rt, [2])
        quantise_h(last, 0, PASS)
        for rt in range(2):
            stage2(1, rt, [3])
        stage2(1, 2, [2, 3])
        stage2(1, 3, range(GROUPS))
        quantise_y(0, 0, 2)
        quantise_y(0, 2, 2)
        store_codes(0, 0, ROW_TILES)
        store_scales(0, [nc.sync])
        for rt in range(3):
            store_y(1, rt)
            round_y(1, rt)
        round_y_from_psum(1, 3)
        store_y(1, 3)
        turn_y(1, 0, 2, scalar_copy)
        turn_y(1, 3, 1, vector_copy)
        turn_y(1, 2, 1, scalar_copy)
        quantise_y(1, 0, 2)
        store_codes(1, 0, 2)
        quantise_y(1, 2, 2)
        store_codes(1, 2, 2)
        store_scales(1, [nc.sync, nc.scalar])
